import numpy as np
import ml_dtypes


def mxq(x, axis, fmt="e4m3"):
    dtype, down = {"e4m3": (ml_dtypes.float8_e4m3fn, 7), "e5m2": (ml_dtypes.float8_e5m2, 14)}[fmt]
    v = np.moveaxis(np.asarray(x, np.float32).astype(ml_dtypes.bfloat16).astype(np.float64), axis, -1)
    blocks = v.reshape(v.shape[:-1] + (-1, 32))
    amax = np.abs(blocks).max(-1, keepdims=True)
    byte = np.maximum(np.where(amax > 0, np.frexp(amax)[1] - 1 + 127, 0) - down, 1)
    scale = np.exp2(byte - 127.0)
    codes = (blocks / scale).astype(np.float32).astype(dtype).astype(np.float64)
    return np.moveaxis((codes * scale).reshape(v.shape), -1, axis)


WIDE = False


def mx_kscale(k):
    if not WIDE:
        return np.ones(k)
    levels = np.array([10, -10, 5, -5, 0])
    if k % 512:
        return np.exp2(np.random.permutation(np.resize(levels, k // 32))).repeat(32)
    a = np.empty((k // 512, 16))
    for p in range(k // 512):
        a[p, :8] = np.random.permutation(np.resize(levels, 8))
        for g in range(8):
            far = levels[np.abs(levels - a[p, g]) >= 10]
            a[p, g + 8] = far[np.random.randint(len(far))]
    return np.exp2(a.ravel()).repeat(32)


BF16 = ml_dtypes.bfloat16


def bf(x):
    return np.asarray(x, np.float32).astype(BF16)


def f64(x):
    return np.asarray(x).astype(np.float64)


E2M1 = np.array([0.0, 0.5, 1.0, 1.5, 2.0, 3.0, 4.0, 6.0, -0.0, -0.5, -1.0, -1.5, -2.0, -3.0, -4.0, -6.0])


def pack_weight(w, fmt):
    k, n = w.shape
    w = f64(bf(w)).reshape(k // 32, 32, n)
    amax = np.abs(w).max(1)
    if fmt == "e4m3":
        byte = np.frexp(amax)[1] - 1 + 127 - 7
    else:
        mant, ex = np.frexp(amax / 6.0)
        byte = np.where(mant > 0.5, ex, ex - 1) + 127
    byte = np.clip(np.where(amax > 0, byte, 1), 1, 254)
    scaled = (w * np.exp2(127.0 - byte)[:, None, :]).reshape(k, n).astype(np.float32)
    by_word = np.ascontiguousarray(scaled.reshape(k // 512, 128, 4, n).transpose(0, 1, 3, 2))
    if fmt == "e4m3":
        words = by_word.astype(ml_dtypes.float8_e4m3fn).view(np.uint8)
    else:
        c = by_word.astype(ml_dtypes.float4_e2m1fn).view(np.uint8) & 0xF
        words = c[..., 0::2] | (c[..., 1::2] << 4)
    return np.ascontiguousarray(words), np.ascontiguousarray(byte.astype(np.uint8).reshape(k // 512, 16, n))


def unpack_weight(words, scales, fmt):
    g, p, n, _ = words.shape
    if fmt == "e4m3":
        vals = np.ascontiguousarray(words).view(ml_dtypes.float8_e4m3fn).astype(np.float64)
    else:
        nib = np.empty((g, p, n, 4), np.uint8)
        nib[..., 0::2] = words & 0xF
        nib[..., 1::2] = words >> 4
        vals = E2M1[nib]
    vals = vals * np.repeat(np.exp2(scales.astype(np.float64) - 127.0), 8, axis=1)[..., None]
    return vals.transpose(0, 1, 3, 2).reshape(g * 512, n)
def pack4(w):
    words, scales = pack_weight(w, "e2m1")
    return words.reshape(words.shape[0], 128, -1), scales


def unpack4(words, scales):
    return unpack_weight(words.reshape(words.shape[0], 128, -1, 2), scales, "e2m1")


def planes(Y):
    n, m = Y.shape
    b = f64(bf(Y)).reshape(n // 32, 32, m)
    amax = np.abs(b).max(1)
    byte = np.clip(np.where(amax > 0, np.frexp(amax)[1] - 1 + 127 - 7, 1), 1, 254)
    codes = (b * np.exp2(127.0 - byte)[:, None, :]).reshape(n, m).astype(np.float32).astype(ml_dtypes.float8_e4m3fn).view(np.uint8)
    words = codes.reshape(n // 512, 128, 4, m).transpose(0, 1, 3, 2)
    return np.ascontiguousarray(words), np.ascontiguousarray(byte.astype(np.uint8).reshape(n // 512, 16, m))


B, N, G, F, C = 32, 8, 512, 1024, 1024

GAMMA = 10.0
CUTOFF = 5.0


def shifted_softplus(t):
    return np.logaddexp(t, 0.0) - np.log(2.0)


def gaussian_basis(dist, mu):
    diff = dist[..., None] - mu
    return np.exp(-GAMMA * np.square(diff))


def cosine_cutoff(dist):
    return 0.5 * (np.cos(np.pi * dist / CUTOFF) + 1.0)


def setup_inputs():
    s, t = mx_kscale(G), mx_kscale(F)
    x = bf(np.random.standard_normal((B, N, C)))
    dist = bf(np.random.uniform(0.5, 4.5, (B, N, N)))
    mu = bf(np.random.uniform(0.0, 5.0, G))
    gr = bf(np.random.standard_normal(G) * s)
    w1_words, w1_scales = pack4(np.random.standard_normal((G, F)) * 5.0 / np.sqrt(G) / s[:, None])
    gf = bf((1.0 + 0.1 * np.random.standard_normal(F)) * t)
    w2_words, w2_scales = pack4(np.random.standard_normal((F, C)) * 1.5 / np.sqrt(F) / t[:, None])
    return {
        "x": x,
        "dist": dist,
        "mu": mu,
        "gr": gr,
        "w1_words": w1_words,
        "w1_scales": w1_scales,
        "gf": gf,
        "w2_words": w2_words,
        "w2_scales": w2_scales,
    }


def core(x, dist, mu, gr, w1_words, w1_scales, gf, w2_words, w2_scales):
    x, dist = f64(x), f64(dist)
    n = x.shape[1]
    rbf = gaussian_basis(dist, f64(mu))
    r = (rbf * f64(gr)).reshape(-1, G)
    h = mxq(r, 1, "e4m3") @ unpack4(w1_words, w1_scales)
    f1 = shifted_softplus(h) * f64(gf)
    filt = mxq(f1, 1, "e4m3") @ unpack4(w2_words, w2_scales)
    filt = filt.reshape(dist.shape + (C,))
    fc = cosine_cutoff(dist)
    messages = x[:, None, :, :] * fc[..., None] * filt
    return np.sum(messages, axis=2) / np.sqrt(n)


def reference(x, dist, mu, gr, w1_words, w1_scales, gf, w2_words, w2_scales):
    R_out = core(x, dist, mu, gr, w1_words, w1_scales, gf, w2_words, w2_scales)
    words, scales = planes(np.moveaxis(R_out, 2, 0).reshape(1024, -1))
    return R_out, words, scales

@@ -1,0 +1,435 @@
+import math
+from contextlib import ExitStack
+
+import concourse.mybir as mybir
+from concourse.masks import make_identity
+
+F32 = mybir.dt.float32
+BF16 = mybir.dt.bfloat16
+I32 = mybir.dt.int32
+U32 = mybir.dt.uint32
+U8 = mybir.dt.uint8
+FP8X4 = mybir.dt.float8_e4m3fn_x4
+FP4X4 = mybir.dt.float4_e2m1fn_x4
+ACT = mybir.ActivationFunctionType
+ALU = mybir.AluOpType
+AX = mybir.AxisListType
+
+B, N, G, F, C = 32, 8, 512, 1024, 1024
+FLOPS = 2 * B * N * N * (G * F + F * C)
+P = 128
+TILES = 16
+GAMMA = 10.0
+PERIOD = 10.0
+LN_FLOOR = 2.0**-40
+CHUNKS = (6, 6, 4)
+PAUSES = (1, 0)
+SIG_START = (3, 3)
+SIG_RATE = (2, 2)
+PROD_BUFS = 6
+ADD_RUN = 2
+LN_AHEAD = 2
+
+
+def tile_schnetfilterinteraction_x2_kernel(
+    tc, x, dist, mu, gr, w1_words, w1_scales, gf, w2_words, w2_scales, out_0, out_1, out_2
+):
+    nc = tc.nc
+    with ExitStack() as ctx:
+        sb = ctx.enter_context(tc.tile_pool(name="sb", bufs=1))
+        ps = ctx.enter_context(tc.psum_pool(name="ps", bufs=1))
+        ctx.enter_context(tc.manual_schedule())
+
+        def sbuf(name, width, dtype):
+            return sb.tile([P, width], dtype, name=name, align_bytes=64)
+
+        def bank(name):
+            return ps.tile([P, 512], F32, name=name)
+
+        sig_banks = [bank("sig0"), bank("sig1")]
+        lin_banks = [bank("lin0"), bank("lin1")]
+        filt_banks = [bank("filt0"), bank("filt1")]
+        sum_banks = [bank("sum0"), bank("sum1")]
+
+        d_sb = sbuf("d_sb", 16, BF16)
+        mu_sb = sbuf("mu_sb", 4, BF16)
+        gr_sb = sbuf("gr_sb", 4, BF16)
+        gf_sb = sbuf("gf_sb", 8, BF16)
+        w1_raw = sbuf("w1_raw", 2048, U8)
+        w1s_raw = sbuf("w1s_raw", 1024, U8)
+        w1_sb = sbuf("w1_sb", 2048, U8)
+        w1s_sb = sbuf("w1s_sb", 1024, U8)
+        w2_sb = sbuf("w2_sb", 4096, U8)
+        w2s_sb = sbuf("w2s_sb", 2048, U8)
+        x_raw = sbuf("x_raw", 2048, BF16)
+        x_sorted = sbuf("x_sorted", 2048, BF16)
+        x_rep = [sbuf("x_rep%d" % q, 4096, BF16) for q in range(4)]
+        ident = sbuf("ident", P, F32)
+        ident_bf = sbuf("ident_bf", P, BF16)
+        row_mask = sbuf("row_mask", 16, F32)
+        d_feat = sbuf("d_feat", P, BF16)
+        mu_feat = sbuf("mu_feat", 4 * P, BF16)
+        mu_rows = sbuf("mu_rows", 4 * P, BF16)
+        d_rows = sbuf("d_rows", TILES * P, BF16)
+        d_sq = sbuf("d_sq", 16, F32)
+        mu_sq = sbuf("mu_sq", 4, F32)
+        turns = sbuf("turns", 16, I32)
+        d_red = sbuf("d_red", 16, F32)
+        sin_d = sbuf("sin_d", 16, F32)
+        sin_sq = sbuf("sin_sq", 16, F32)
+        fc = sbuf("fc", 16, F32)
+        neg_gr = sbuf("neg_gr", 4, F32)
+        neg_gf = sbuf("neg_gf", 8, F32)
+        work = [sbuf("work%d" % k, 1024, F32) for k in range(TILES)]
+        r_bf = [sbuf("r_bf%d" % k, 512, BF16) for k in range(2)]
+        r_codes = sbuf("r_codes", TILES * P, U32)
+        r_scales = sbuf("r_scales", TILES * P, U8)
+        f1_bf = sbuf("f1_bf", 1024, BF16)
+        f1_codes = [sbuf("f1_codes%d" % k, 256, U32) for k in range(2)]
+        f1_scales = [sbuf("f1_scales%d" % k, 256, U8) for k in range(2)]
+        prod = [[sbuf("prod%d_%d" % (k, ch), 512, F32) for ch in range(2)] for k in range(PROD_BUFS)]
+        y_t = [sbuf("y_t%d" % k, 512, F32) for k in range(2)]
+        y_bf = [sbuf("y_bf%d" % k, 512, BF16) for k in range(2)]
+        y_sb = [sbuf("y_sb%d" % k, 512, F32) for k in range(4)]
+        y_codes = [sbuf("y_codes%d" % k, 256, U32) for k in range(2)]
+        y_scales = sbuf("y_scales", 512, U8)
+
+        out_rows = out_0.rearrange("b i c -> (b i) c")
+        park = out_rows[P : 2 * P, :].bitcast(BF16)
+
+        nc.sync.dma_start(
+            out=d_sb[:].rearrange("p (h j) -> p h j", h=2),
+            in_=dist.rearrange("b i j -> (b i) j").rearrange("(h p) j -> p h j", h=2),
+        )
+        nc.sync.dma_start(out=mu_sb[:], in_=mu.rearrange("(p t) -> p t", t=4))
+        nc.sync.dma_start(out=gr_sb[:], in_=gr.rearrange("(p t) -> p t", t=4))
+        nc.sync.dma_start(out=x_raw[:], in_=x.rearrange("b j c -> (b j) c").rearrange("(p e) c -> p (e c)", e=2))
+        nc.sync.dma_start(out=w1_raw[:].bitcast(I32), in_=w1_words[0].bitcast(I32))
+        nc.vector.memset(w1s_raw[:].bitcast(I32), 0)
+        nc.vector.memset(d_feat[:, 48:80], 1.0)
+        nc.vector.memset(d_feat[:, 80:128], 0.0)
+        mu_feat3 = mu_feat[:].rearrange("p (t s) -> p t s", t=4)
+        nc.vector.memset(mu_feat3[:, :, 16:48], 1.0)
+        nc.vector.memset(mu_feat3[:, :, 80:128], 0.0)
+        nc.vector.memset(w2s_sb[:].bitcast(I32), 0)
+        for q in range(4):
+            nc.sync.dma_start(
+                out=w1s_raw[32 * q : 32 * q + 4, :].bitcast(I32), in_=w1_scales[0, 4 * q : 4 * q + 4, :].bitcast(I32)
+            )
+        nc.sync.dma_start(
+            out=gf_sb[:].rearrange("p (g t) -> p g t", g=2), in_=gf.rearrange("(g p t) -> p g t", g=2, t=4)
+        )
+        for q in range(4):
+            nc.sync.dma_start(
+                out=w2s_sb[32 * q : 32 * q + 4, :].rearrange("r (g n) -> r g n", g=2).bitcast(I32),
+                in_=w2_scales[:, 4 * q : 4 * q + 4, :].rearrange("g r n -> r g n").bitcast(I32),
+            )
+        nc.sync.dma_start(
+            out=w2_sb[:].rearrange("p (g n) -> p g n", g=2).bitcast(I32),
+            in_=w2_words.rearrange("g p n -> p g n").bitcast(I32),
+        )
+        make_identity(nc, ident_bf[:])
+        make_identity(nc, ident[:])
+
+        nc.vector.tensor_scalar(out=turns[:], in0=d_sb[:], scalar1=1.0 / PERIOD, scalar2=None, op0=ALU.mult)
+        nc.vector.scalar_tensor_tensor(
+            out=d_red[:], in0=turns[:], scalar=-PERIOD, in1=d_sb[:], op0=ALU.mult, op1=ALU.add
+        )
+        nc.scalar.activation(out=sin_d[:], in_=d_red[:], func=ACT.Sin, scale=math.pi / PERIOD)
+
+        nc.vector.tensor_tensor(out=d_sq[:], in0=d_sb[:], in1=d_sb[:], op=ALU.mult)
+        nc.vector.tensor_tensor(out=mu_sq[:], in0=mu_sb[:], in1=mu_sb[:], op=ALU.mult)
+        nc.vector.tensor_copy(out=d_feat[:, 0:16], in_=d_sb[:])
+        nc.vector.tensor_copy(out=d_feat[:, 16:32], in_=d_sq[:])
+        mu_wide = mu_sb[:].unsqueeze(2).to_broadcast([P, 4, 16])
+        mu_sq_wide = mu_sq[:].unsqueeze(2).to_broadcast([P, 4, 16])
+        nc.vector.tensor_copy(out=mu_feat3[:, :, 48:64], in_=mu_sq_wide)
+        nc.vector.tensor_tensor(out=d_feat[:, 32:48], in0=d_sq[:], in1=d_feat[:, 16:32], op=ALU.subtract)
+        nc.vector.tensor_scalar(out=mu_feat3[:, :, 0:16], in0=mu_wide, scalar1=-2.0, scalar2=None, op0=ALU.mult)
+        nc.vector.tensor_tensor(out=mu_feat3[:, :, 64:80], in0=mu_sq_wide, in1=mu_feat3[:, :, 48:64], op=ALU.subtract)
+        nc.vector.tensor_reduce(
+            out=row_mask[:], in_=ident_bf[:].rearrange("p (k s) -> p s k", s=16), axis=AX.X, op=ALU.add
+        )
+        d_t = filt_banks[0][:].bitcast(BF16)
+        mu_t = filt_banks[1][:].bitcast(BF16)
+        nc.tensor.transpose(d_t[:, 0:P], d_feat[:], ident_bf[:])
+        for t in range(4):
+            nc.tensor.transpose(mu_t[:, t * P : (t + 1) * P], mu_feat[:, t * P : (t + 1) * P], ident_bf[:])
+        nc.vector.tensor_scalar(out=neg_gr[:], in0=gr_sb[:], scalar1=-1.0, scalar2=None, op0=ALU.mult)
+        nc.vector.tensor_copy(out=mu_rows[:], in_=mu_t[:, 0 : 4 * P])
+        for k in range(TILES):
+            nc.vector.tensor_scalar(
+                out=d_rows[:, k * P : (k + 1) * P],
+                in0=d_t[:, 0:P],
+                scalar1=row_mask[:, k : k + 1],
+                scalar2=None,
+                op0=ALU.mult,
+            )
+
+        def words_last(ap):
+            return ap.rearrange("p (t n) -> p n t", t=4)
+
+        def words(ap):
+            return ap.rearrange("p (n t) -> p n t", t=4)
+
+        gauss_banks = sig_banks + lin_banks
+        for k in range(TILES):
+            sq = gauss_banks[k % 4]
+            for t in range(4):
+                nc.tensor.matmul(
+                    sq[:, t * P : (t + 1) * P],
+                    lhsT=mu_rows[:, t * P : (t + 1) * P],
+                    rhs=d_rows[:, k * P : (k + 1) * P],
+                    start=True,
+                    stop=True,
+                )
+            nc.scalar.activation(out=words(work[k][:, 0:512]), in_=words_last(sq[:]), func=ACT.Exp, scale=-GAMMA)
+
+        def r_gain(k):
+            nc.vector.tensor_tensor(
+                out=words(r_bf[k % 2][:]),
+                in0=words(work[k][:, 0:512]),
+                in1=neg_gr[:].unsqueeze(1).to_broadcast([P, P, 4]),
+                op=ALU.mult,
+            )
+
+        def r_quantize(k):
+            cols = slice(k * P, (k + 1) * P)
+            nc.vector.quantize_mx(out=r_codes[:, cols].bitcast(FP8X4), scales=r_scales[:, cols], in_=r_bf[k % 2][:])
+
+        def r_tiles(first, last):
+            r_gain(first)
+            for k in range(first, last):
+                if k + 1 < last:
+                    r_gain(k + 1)
+                r_quantize(k)
+
+        nc.vector.tensor_copy(
+            out=w1_sb[:].rearrange("p (g t m b) -> p g t m b", g=2, t=4, b=2),
+            in_=w1_raw[:].rearrange("p (g m t b) -> p g t m b", g=2, t=4, b=2),
+        )
+        r_tiles(0, CHUNKS[0])
+        nc.vector.tensor_copy(
+            out=w1s_sb[:].rearrange("p (g t m) -> p g t m", g=2, t=4),
+            in_=w1s_raw[:].rearrange("p (g m t) -> p g t m", g=2, t=4),
+        )
+        nc.vector.tensor_copy(
+            out=x_sorted[:].rearrange("p (g t m) -> p g t m", g=4, t=4),
+            in_=x_raw[:].rearrange("p (g m t) -> p g t m", g=4, t=4),
+        )
+        nc.sync.dma_start(out=park, in_=x_sorted[:])
+        park_b = park.rearrange("(b r) n -> b (r n)", r=4)
+        for q in range(4):
+            h, jh = divmod(q, 2)
+            nc.sync.dma_start(
+                out=x_rep[q][:],
+                in_=park_b[16 * h : 16 * h + 16, 4096 * jh : 4096 * (jh + 1)].unsqueeze(1).to_broadcast([16, 8, 4096]),
+            )
+        nc.vector.tensor_tensor(out=sin_sq[:], in0=sin_d[:], in1=sin_d[:], op=ALU.mult)
+        nc.vector.tensor_scalar(out=neg_gf[:], in0=gf_sb[:], scalar1=-1.0, scalar2=None, op0=ALU.mult)
+        nc.vector.tensor_scalar(
+            out=fc[:], in0=sin_sq[:], scalar1=-1.0 / math.sqrt(N), scalar2=1.0 / math.sqrt(N), op0=ALU.mult, op1=ALU.add
+        )
+        r_tiles(CHUNKS[0], TILES)
+
+        def first_matmul(k, g, dst):
+            cols = slice(k * P, (k + 1) * P)
+            for t in range(4):
+                s = 4 * g + t
+                nc.tensor.matmul_mx(
+                    out=dst[:, t * P : (t + 1) * P],
+                    lhsT=w1_sb[:, 2 * P * s : 2 * P * (s + 1)].bitcast(FP4X4),
+                    lhsT_scale=w1s_sb[:, P * s : P * (s + 1)],
+                    rhs=r_codes[:, cols].bitcast(FP8X4),
+                    rhs_scale=r_scales[:, cols],
+                    start=True,
+                    stop=True,
+                )
+
+        def sigmoid_half(k, g):
+            first_matmul(k, g, sig_banks[g])
+            nc.scalar.activation(
+                out=words(work[k][:, 512 * g : 512 * (g + 1)]), in_=words_last(sig_banks[g][:]), func=ACT.Sigmoid
+            )
+
+        def log_pass(k):
+            nc.scalar.activation(out=work[k][:], in_=work[k][:], func=ACT.Ln, scale=2.0, bias=LN_FLOOR)
+
+        def again(k, g):
+            first_matmul(k, g, lin_banks[g])
+
+        def guard(k):
+            for g in range(2):
+                half = words(work[k][:, 512 * g : 512 * (g + 1)])
+                nc.vector.scalar_tensor_tensor(
+                    out=half, in0=words_last(lin_banks[g][:]), scalar=math.log(2.0), in1=half, op0=ALU.add, op1=ALU.min
+                )
+
+        def f1_gain(k, engine):
+            engine.tensor_tensor(
+                out=f1_bf[:].rearrange("p (g n t) -> p g n t", g=2, t=4),
+                in0=work[k][:].rearrange("p (g n t) -> p g n t", g=2, t=4),
+                in1=neg_gf[:].rearrange("p (g t) -> p g t", g=2).unsqueeze(2).to_broadcast([P, 2, P, 4]),
+                op=ALU.mult,
+            )
+
+        def f1_quantize(k):
+            nc.vector.quantize_mx(out=f1_codes[k % 2][:].bitcast(FP8X4), scales=f1_scales[k % 2][:], in_=f1_bf[:])
+
+        def second_matmul(k, ch):
+            dst = (lin_banks if k == TILES - 1 else filt_banks)[ch]
+            for g in range(2):
+                nc.tensor.matmul_mx(
+                    out=dst[:],
+                    lhsT=f1_codes[k % 2][:, P * g : P * (g + 1)].bitcast(FP8X4),
+                    lhsT_scale=f1_scales[k % 2][:, P * g : P * (g + 1)],
+                    rhs=w2_sb[:, 2048 * g + 1024 * ch : 2048 * g + 1024 * (ch + 1)].bitcast(FP4X4),
+                    rhs_scale=w2s_sb[:, 1024 * g + 512 * ch : 1024 * g + 512 * (ch + 1)],
+                    start=(g == 0),
+                    stop=(g == 1),
+                )
+
+        def message(k):
+            src = lin_banks if k == TILES - 1 else filt_banks
+            for ch in range(2):
+                x0 = 1024 * (k % 4) + 512 * ch
+                nc.vector.scalar_tensor_tensor(
+                    out=prod[k % PROD_BUFS][ch][:].rearrange("p (t m) -> p t m", t=4),
+                    in0=src[ch][:].rearrange("p (m t) -> p t m", t=4),
+                    scalar=fc[:, k : k + 1],
+                    in1=x_rep[k // 4][:, x0 : x0 + 512].rearrange("p (t m) -> p t m", t=4),
+                    op0=ALU.mult,
+                    op1=ALU.mult,
+                )
+
+        def add_up(k):
+            j = k % N
+            for ch in range(2):
+                for t in range(4):
+                    nc.tensor.matmul(
+                        sum_banks[ch][:, t * P : (t + 1) * P],
+                        lhsT=prod[k % PROD_BUFS][ch][:, P * t : P * (t + 1)],
+                        rhs=ident[:],
+                        is_transpose=True,
+                        start=(j == 0 and t == 0),
+                        stop=(j == N - 1 and t == 3),
+                    )
+
+        def sums_out():
+            for ch in range(2):
+                nc.scalar.copy(out=y_t[ch][:], in_=sum_banks[ch][:])
+                nc.scalar.copy(out=words(y_bf[ch][:]), in_=words_last(sum_banks[ch][:]))
+
+        def last_sums_out():
+            nc.scalar.copy(out=y_t[0][:], in_=sum_banks[0][:])
+            nc.vector.tensor_copy(out=y_t[1][:], in_=sum_banks[1][:])
+            for ch in range(2):
+                nc.vector.tensor_copy(out=words(y_bf[ch][:]), in_=words_last(y_t[ch][:]))
+
+        def store_rows(h):
+            for ch in range(2):
+                for t in range(4):
+                    nc.tensor.transpose(sig_banks[ch][:, t * P : (t + 1) * P], y_t[ch][:, t * P : (t + 1) * P], ident[:])
+                rows = y_sb[2 * h + ch]
+                nc.scalar.copy(out=words(rows[:]), in_=words_last(sig_banks[ch][:]))
+                nc.sync.dma_start(out=out_rows[P * h : P * (h + 1), 512 * ch : 512 * (ch + 1)], in_=rows[:])
+
+        def store_codes(h):
+            for ch in range(2):
+                s0 = 256 * ch + P * h
+                nc.vector.quantize_mx(
+                    out=y_codes[h][:, P * ch : P * (ch + 1)].bitcast(FP8X4), scales=y_scales[:, s0 : s0 + P], in_=y_bf[ch][:]
+                )
+            nc.sync.dma_start(
+                out=out_1[:, :, P * h : P * (h + 1), :].rearrange("g p m t -> p g (m t)").bitcast(I32),
+                in_=y_codes[h][:].rearrange("p (g m) -> p g m", g=2).bitcast(I32),
+            )
+
+        starts = [sum(CHUNKS[:c]) for c in range(len(CHUNKS) + 1)]
+        front = []
+        sig_at = {}
+        for c in range(len(CHUNKS)):
+            if c + 1 < len(CHUNKS):
+                for n, k in enumerate(range(starts[c + 1], starts[c + 2])):
+                    sig_at.setdefault(len(front) + SIG_START[c] + n // SIG_RATE[c], []).append(k)
+            front.extend(range(starts[c], starts[c + 1]))
+            if c < len(PAUSES):
+                front.extend([None] * PAUSES[c])
+        front.append(None)
+        last_chunk = starts[-2]
+
+        for k in range(CHUNKS[0]):
+            for g in range(2):
+                sigmoid_half(k, g)
+        for g in range(2):
+            again(0, g)
+        for k in range(CHUNKS[0]):
+            log_pass(k)
+
+        def at(s):
+            return front[s] if s >= 0 else None
+
+        added = 0
+        made = 0
+        rows_due = -2
+        for s in range(len(front)):
+            v, p, q = at(s), at(s - 1), at(s - 2)
+            sig = sig_at.get(s, [])
+            if q is not None:
+                f1_quantize(q)
+            if rows_due + 1 == s:
+                store_codes(0)
+            if p == TILES - 1:
+                f1_gain(p, nc.vector)
+            elif p is not None:
+                f1_gain(p, nc.gpsimd)
+            if v is not None:
+                if v >= last_chunk and v + LN_AHEAD < TILES:
+                    log_pass(v + LN_AHEAD)
+                guard(v)
+            halves = [(k, g) for k in sig for g in range(2)]
+            others = []
+            if q is not None:
+                others.extend([(second_matmul, q, 0), (second_matmul, q, 1)])
+            if v is not None and v + 1 < TILES:
+                others.extend([(again, v + 1, 0), (again, v + 1, 1)])
+            for n in range(max(len(halves), len(others))):
+                if n < len(halves):
+                    sigmoid_half(*halves[n])
+                if n < len(others):
+                    others[n][0](*others[n][1:])
+            if sig and sig[-1] + 1 in starts:
+                first = starts[starts.index(sig[-1] + 1) - 1]
+                last = first + LN_AHEAD if first == last_chunk else sig[-1] + 1
+                for k in range(first, last):
+                    log_pass(k)
+            if rows_due == s:
+                store_rows(0)
+            ending = p == TILES - 1
+            if not sig and (made - added >= ADD_RUN or ending) and rows_due != s:
+                stop = made if ending else added + ADD_RUN
+                for k in range(added, stop):
+                    add_up(k)
+                added = stop
+                if added == N:
+                    sums_out()
+                    rows_due = s + 1
+            if ending:
+                f1_quantize(p)
+                for ch in range(2):
+                    second_matmul(p, ch)
+            if q is not None:
+                message(q)
+                made = q + 1
+
+        add_up(TILES - 2)
+        message(TILES - 1)
+        add_up(TILES - 1)
+        last_sums_out()
+        store_codes(1)
+        store_rows(1)
+        for q in range(4):
+            nc.scalar.dma_start(
+                out=out_2[:, 4 * q : 4 * q + 4, :].rearrange("g r m -> r g m").bitcast(I32),
+                in_=y_scales[32 * q : 32 * q + 4, :].rearrange("r (g m) -> r g m", g=2).bitcast(I32),
+            )

@@ -24,8 +24,10 @@ PERIOD = 10.0
 LN_FLOOR = 2.0**-40
 CHUNKS = (6, 6, 4)
 PAUSES = (1, 0)
-SIG_START = (3, 3)
-SIG_RATE = (2, 2)
+SIG_START = (2, 2)
+SIG_RATE = 2
+SIG_LEAD = 1
+POOL_COLS = 768
 PROD_BUFS = 6
 ADD_RUN = 2
 LN_AHEAD = 2
@@ -79,7 +81,7 @@ def tile_schnetfilterinteraction_x2_kernel(
         sin_sq = sbuf("sin_sq", 16, F32)
         fc = sbuf("fc", 16, F32)
         neg_gr = sbuf("neg_gr", 4, F32)
-        neg_gf = sbuf("neg_gf", 8, F32)
+        neg_gf = sbuf("neg_gf", 1024, F32)
         work = [sbuf("work%d" % k, 1024, F32) for k in range(TILES)]
         r_bf = [sbuf("r_bf%d" % k, 512, BF16) for k in range(2)]
         r_codes = sbuf("r_codes", TILES * P, U32)
@@ -226,11 +228,22 @@ def tile_schnetfilterinteraction_x2_kernel(
                 in_=park_b[16 * h : 16 * h + 16, 4096 * jh : 4096 * (jh + 1)].unsqueeze(1).to_broadcast([16, 8, 4096]),
             )
         nc.vector.tensor_tensor(out=sin_sq[:], in0=sin_d[:], in1=sin_d[:], op=ALU.mult)
-        nc.vector.tensor_scalar(out=neg_gf[:], in0=gf_sb[:], scalar1=-1.0, scalar2=None, op0=ALU.mult)
+        nc.vector.tensor_scalar(
+            out=neg_gf[:].rearrange("p (g n t) -> p g n t", g=2, t=4),
+            in0=gf_sb[:].rearrange("p (g t) -> p g t", g=2).unsqueeze(2).to_broadcast([P, 2, P, 4]),
+            scalar1=-1.0,
+            scalar2=None,
+            op0=ALU.mult,
+        )
         nc.vector.tensor_scalar(
             out=fc[:], in0=sin_sq[:], scalar1=-1.0 / math.sqrt(N), scalar2=1.0 / math.sqrt(N), op0=ALU.mult, op1=ALU.add
         )
         r_tiles(CHUNKS[0], TILES)
+
+        starts = [sum(CHUNKS[:c]) for c in range(len(CHUNKS) + 1)]
+
+        def first_last(c):
+            return list(range(starts[c] + 1, starts[c + 1])) + [starts[c]]
 
         def first_matmul(k, g, dst):
             cols = slice(k * P, (k + 1) * P)
@@ -259,19 +272,15 @@ def tile_schnetfilterinteraction_x2_kernel(
             first_matmul(k, g, lin_banks[g])
 
         def guard(k):
+            src = sig_banks if k in starts else lin_banks
             for g in range(2):
                 half = words(work[k][:, 512 * g : 512 * (g + 1)])
                 nc.vector.scalar_tensor_tensor(
-                    out=half, in0=words_last(lin_banks[g][:]), scalar=math.log(2.0), in1=half, op0=ALU.add, op1=ALU.min
+                    out=half, in0=words_last(src[g][:]), scalar=math.log(2.0), in1=half, op0=ALU.add, op1=ALU.min
                 )
 
-        def f1_gain(k, engine):
-            engine.tensor_tensor(
-                out=f1_bf[:].rearrange("p (g n t) -> p g n t", g=2, t=4),
-                in0=work[k][:].rearrange("p (g n t) -> p g n t", g=2, t=4),
-                in1=neg_gf[:].rearrange("p (g t) -> p g t", g=2).unsqueeze(2).to_broadcast([P, 2, P, 4]),
-                op=ALU.mult,
-            )
+        def f1_gain(k, engine, cols):
+            engine.tensor_tensor(out=f1_bf[:, cols], in0=work[k][:, cols], in1=neg_gf[:, cols], op=ALU.mult)
 
         def f1_quantize(k):
             nc.vector.quantize_mx(out=f1_codes[k % 2][:].bitcast(FP8X4), scales=f1_scales[k % 2][:], in_=f1_bf[:])
@@ -345,44 +354,54 @@ def tile_schnetfilterinteraction_x2_kernel(
                 in_=y_codes[h][:].rearrange("p (g m) -> p g m", g=2).bitcast(I32),
             )
 
-        starts = [sum(CHUNKS[:c]) for c in range(len(CHUNKS) + 1)]
         front = []
         sig_at = {}
         for c in range(len(CHUNKS)):
             if c + 1 < len(CHUNKS):
-                for n, k in enumerate(range(starts[c + 1], starts[c + 2])):
-                    sig_at.setdefault(len(front) + SIG_START[c] + n // SIG_RATE[c], []).append(k)
+                for n, k in enumerate(first_last(c + 1)):
+                    sig_at.setdefault(len(front) + SIG_START[c] + (n + SIG_LEAD) // SIG_RATE, []).append(k)
             front.extend(range(starts[c], starts[c + 1]))
             if c < len(PAUSES):
                 front.extend([None] * PAUSES[c])
         front.append(None)
         last_chunk = starts[-2]
 
-        for k in range(CHUNKS[0]):
+        for k in first_last(0):
             for g in range(2):
                 sigmoid_half(k, g)
         for g in range(2):
-            again(0, g)
+            again(1, g)
         for k in range(CHUNKS[0]):
             log_pass(k)
 
         def at(s):
             return front[s] if s >= 0 else None
 
+        pool_cols = slice(0, POOL_COLS)
+        rest_cols = slice(POOL_COLS, 1024)
         added = 0
         made = 0
         rows_due = -2
         for s in range(len(front)):
             v, p, q = at(s), at(s - 1), at(s - 2)
             sig = sig_at.get(s, [])
-            if q is not None:
-                f1_quantize(q)
             if rows_due + 1 == s:
                 store_codes(0)
+            if q is not None:
+                if q < TILES - 2:
+                    f1_gain(q, nc.vector, rest_cols)
+                f1_quantize(q)
             if p == TILES - 1:
-                f1_gain(p, nc.vector)
+                f1_gain(p, nc.vector, slice(0, 1024))
+            elif p == TILES - 2:
+                f1_gain(p, nc.gpsimd, slice(0, 1024))
             elif p is not None:
-                f1_gain(p, nc.gpsimd)
+                f1_gain(p, nc.gpsimd, pool_cols)
+            ending = p == TILES - 1
+            if ending:
+                for k in range(added, made):
+                    add_up(k)
+                added = made
             if v is not None:
                 if v >= last_chunk and v + LN_AHEAD < TILES:
                     log_pass(v + LN_AHEAD)
@@ -391,33 +410,34 @@ def tile_schnetfilterinteraction_x2_kernel(
             others = []
             if q is not None:
                 others.extend([(second_matmul, q, 0), (second_matmul, q, 1)])
-            if v is not None and v + 1 < TILES:
-                others.extend([(again, v + 1, 0), (again, v + 1, 1)])
+            if v is not None and v not in starts and v + 1 < TILES:
+                nxt = v + 2 if v + 1 in starts else v + 1
+                others.extend([(again, nxt, 0), (again, nxt, 1)])
             for n in range(max(len(halves), len(others))):
-                if n < len(halves):
-                    sigmoid_half(*halves[n])
                 if n < len(others):
                     others[n][0](*others[n][1:])
-            if sig and sig[-1] + 1 in starts:
-                first = starts[starts.index(sig[-1] + 1) - 1]
-                last = first + LN_AHEAD if first == last_chunk else sig[-1] + 1
+                if n < len(halves):
+                    sigmoid_half(*halves[n])
+            if sig and sig[-1] in starts:
+                first = sig[-1]
+                last = first + LN_AHEAD if first == last_chunk else starts[starts.index(first) + 1]
                 for k in range(first, last):
                     log_pass(k)
             if rows_due == s:
                 store_rows(0)
-            ending = p == TILES - 1
-            if not sig and (made - added >= ADD_RUN or ending) and rows_due != s:
-                stop = made if ending else added + ADD_RUN
+            if ending:
+                f1_quantize(p)
+                for ch in range(2):
+                    second_matmul(p, ch)
+            flush = s == len(front) - 2
+            if not sig and not ending and (made - added >= ADD_RUN or flush) and rows_due != s:
+                stop = made if flush else added + ADD_RUN
                 for k in range(added, stop):
                     add_up(k)
                 added = stop
                 if added == N:
                     sums_out()
                     rows_due = s + 1
-            if ending:
-                f1_quantize(p)
-                for ch in range(2):
-                    second_matmul(p, ch)
             if q is not None:
                 message(q)
                 made = q + 1

@@ -23,11 +23,9 @@ GAMMA = 10.0
 PERIOD = 10.0
 LN_FLOOR = 2.0**-40
 CHUNKS = (6, 6, 4)
-PAUSES = (1, 0)
 SIG_START = (2, 2)
 SIG_RATE = 2
 SIG_LEAD = 1
-POOL_COLS = 768
 PROD_BUFS = 6
 ADD_RUN = 2
 LN_AHEAD = 2
@@ -63,8 +61,6 @@ def tile_schnetfilterinteraction_x2_kernel(
         w1s_sb = sbuf("w1s_sb", 1024, U8)
         w2_sb = sbuf("w2_sb", 4096, U8)
         w2s_sb = sbuf("w2s_sb", 2048, U8)
-        x_raw = sbuf("x_raw", 2048, BF16)
-        x_sorted = sbuf("x_sorted", 2048, BF16)
         x_rep = [sbuf("x_rep%d" % q, 4096, BF16) for q in range(4)]
         ident = sbuf("ident", P, F32)
         ident_bf = sbuf("ident_bf", P, BF16)
@@ -86,18 +82,18 @@ def tile_schnetfilterinteraction_x2_kernel(
         r_bf = [sbuf("r_bf%d" % k, 512, BF16) for k in range(2)]
         r_codes = sbuf("r_codes", TILES * P, U32)
         r_scales = sbuf("r_scales", TILES * P, U8)
-        f1_bf = sbuf("f1_bf", 1024, BF16)
+        f1_bf = [sbuf("f1_bf%d" % k, 1024, BF16) for k in range(2)]
         f1_codes = [sbuf("f1_codes%d" % k, 256, U32) for k in range(2)]
         f1_scales = [sbuf("f1_scales%d" % k, 256, U8) for k in range(2)]
         prod = [[sbuf("prod%d_%d" % (k, ch), 512, F32) for ch in range(2)] for k in range(PROD_BUFS)]
         y_t = [sbuf("y_t%d" % k, 512, F32) for k in range(2)]
         y_bf = [sbuf("y_bf%d" % k, 512, BF16) for k in range(2)]
+        y_words = [sbuf("y_words%d" % k, 512, BF16) for k in range(2)]
         y_sb = [sbuf("y_sb%d" % k, 512, F32) for k in range(4)]
         y_codes = [sbuf("y_codes%d" % k, 256, U32) for k in range(2)]
         y_scales = sbuf("y_scales", 512, U8)
 
         out_rows = out_0.rearrange("b i c -> (b i) c")
-        park = out_rows[P : 2 * P, :].bitcast(BF16)
 
         nc.sync.dma_start(
             out=d_sb[:].rearrange("p (h j) -> p h j", h=2),
@@ -105,7 +101,6 @@ def tile_schnetfilterinteraction_x2_kernel(
         )
         nc.sync.dma_start(out=mu_sb[:], in_=mu.rearrange("(p t) -> p t", t=4))
         nc.sync.dma_start(out=gr_sb[:], in_=gr.rearrange("(p t) -> p t", t=4))
-        nc.sync.dma_start(out=x_raw[:], in_=x.rearrange("b j c -> (b j) c").rearrange("(p e) c -> p (e c)", e=2))
         nc.sync.dma_start(out=w1_raw[:].bitcast(I32), in_=w1_words[0].bitcast(I32))
         nc.vector.memset(w1s_raw[:].bitcast(I32), 0)
         nc.vector.memset(d_feat[:, 48:80], 1.0)
@@ -130,6 +125,13 @@ def tile_schnetfilterinteraction_x2_kernel(
             out=w2_sb[:].rearrange("p (g n) -> p g n", g=2).bitcast(I32),
             in_=w2_words.rearrange("g p n -> p g n").bitcast(I32),
         )
+        x_b = x.rearrange("b j c -> b (j c)")
+        for q in range(4):
+            h, jh = divmod(q, 2)
+            nc.sync.dma_start(
+                out=x_rep[q][:],
+                in_=x_b[16 * h : 16 * h + 16, 4096 * jh : 4096 * (jh + 1)].unsqueeze(1).to_broadcast([16, 8, 4096]),
+            )
         make_identity(nc, ident_bf[:])
         make_identity(nc, ident[:])
 
@@ -215,18 +217,6 @@ def tile_schnetfilterinteraction_x2_kernel(
             out=w1s_sb[:].rearrange("p (g t m) -> p g t m", g=2, t=4),
             in_=w1s_raw[:].rearrange("p (g m t) -> p g t m", g=2, t=4),
         )
-        nc.vector.tensor_copy(
-            out=x_sorted[:].rearrange("p (g t m) -> p g t m", g=4, t=4),
-            in_=x_raw[:].rearrange("p (g m t) -> p g t m", g=4, t=4),
-        )
-        nc.sync.dma_start(out=park, in_=x_sorted[:])
-        park_b = park.rearrange("(b r) n -> b (r n)", r=4)
-        for q in range(4):
-            h, jh = divmod(q, 2)
-            nc.sync.dma_start(
-                out=x_rep[q][:],
-                in_=park_b[16 * h : 16 * h + 16, 4096 * jh : 4096 * (jh + 1)].unsqueeze(1).to_broadcast([16, 8, 4096]),
-            )
         nc.vector.tensor_tensor(out=sin_sq[:], in0=sin_d[:], in1=sin_d[:], op=ALU.mult)
         nc.vector.tensor_scalar(
             out=neg_gf[:].rearrange("p (g n t) -> p g n t", g=2, t=4),
@@ -279,14 +269,14 @@ def tile_schnetfilterinteraction_x2_kernel(
                     out=half, in0=words_last(src[g][:]), scalar=math.log(2.0), in1=half, op0=ALU.add, op1=ALU.min
                 )
 
-        def f1_gain(k, engine, cols):
-            engine.tensor_tensor(out=f1_bf[:, cols], in0=work[k][:, cols], in1=neg_gf[:, cols], op=ALU.mult)
+        def f1_gain(k, buf):
+            nc.gpsimd.tensor_tensor(out=f1_bf[buf][:], in0=work[k][:], in1=neg_gf[:], op=ALU.mult)
 
-        def f1_quantize(k):
-            nc.vector.quantize_mx(out=f1_codes[k % 2][:].bitcast(FP8X4), scales=f1_scales[k % 2][:], in_=f1_bf[:])
+        def f1_quantize(k, buf):
+            nc.vector.quantize_mx(out=f1_codes[k % 2][:].bitcast(FP8X4), scales=f1_scales[k % 2][:], in_=f1_bf[buf][:])
 
         def second_matmul(k, ch):
-            dst = (lin_banks if k == TILES - 1 else filt_banks)[ch]
+            dst = (lin_banks if k == TILES - 2 else filt_banks)[ch]
             for g in range(2):
                 nc.tensor.matmul_mx(
                     out=dst[:],
@@ -299,14 +289,14 @@ def tile_schnetfilterinteraction_x2_kernel(
                 )
 
         def message(k):
-            src = lin_banks if k == TILES - 1 else filt_banks
+            src = lin_banks if k == TILES - 2 else filt_banks
             for ch in range(2):
                 x0 = 1024 * (k % 4) + 512 * ch
                 nc.vector.scalar_tensor_tensor(
-                    out=prod[k % PROD_BUFS][ch][:].rearrange("p (t m) -> p t m", t=4),
-                    in0=src[ch][:].rearrange("p (m t) -> p t m", t=4),
+                    out=prod[k % PROD_BUFS][ch][:],
+                    in0=src[ch][:],
                     scalar=fc[:, k : k + 1],
-                    in1=x_rep[k // 4][:, x0 : x0 + 512].rearrange("p (t m) -> p t m", t=4),
+                    in1=x_rep[k // 4][:, x0 : x0 + 512],
                     op0=ALU.mult,
                     op1=ALU.mult,
                 )
@@ -324,30 +314,34 @@ def tile_schnetfilterinteraction_x2_kernel(
                         stop=(j == N - 1 and t == 3),
                     )
 
-        def sums_out():
+        def sums_out(copies):
             for ch in range(2):
-                nc.scalar.copy(out=y_t[ch][:], in_=sum_banks[ch][:])
-                nc.scalar.copy(out=words(y_bf[ch][:]), in_=words_last(sum_banks[ch][:]))
+                copies[ch](out=y_t[ch][:], in_=sum_banks[ch][:])
 
-        def last_sums_out():
-            nc.scalar.copy(out=y_t[0][:], in_=sum_banks[0][:])
-            nc.vector.tensor_copy(out=y_t[1][:], in_=sum_banks[1][:])
-            for ch in range(2):
-                nc.vector.tensor_copy(out=words(y_bf[ch][:]), in_=words_last(y_t[ch][:]))
+        def store_rows(h, ch):
+            for t in range(4):
+                nc.tensor.transpose(sig_banks[ch][:, t * P : (t + 1) * P], y_t[ch][:, t * P : (t + 1) * P], ident[:])
+            rows = y_sb[2 * h + ch]
+            nc.scalar.copy(out=rows[:], in_=sig_banks[ch][:])
+            nc.sync.dma_start(out=out_rows[P * h : P * (h + 1), 512 * ch : 512 * (ch + 1)], in_=rows[:])
 
-        def store_rows(h):
-            for ch in range(2):
-                for t in range(4):
-                    nc.tensor.transpose(sig_banks[ch][:, t * P : (t + 1) * P], y_t[ch][:, t * P : (t + 1) * P], ident[:])
-                rows = y_sb[2 * h + ch]
-                nc.scalar.copy(out=words(rows[:]), in_=words_last(sig_banks[ch][:]))
-                nc.sync.dma_start(out=out_rows[P * h : P * (h + 1), 512 * ch : 512 * (ch + 1)], in_=rows[:])
+        def round_rows(h, ch, copy):
+            copy(out=y_bf[ch][:], in_=y_sb[2 * h + ch][:])
+
+        def turn_words(ch, copy):
+            pairs = y_bf[ch][:].bitcast(F32)
+            for u in range(2):
+                nc.tensor.transpose(sig_banks[ch][:, u * P : (u + 1) * P], pairs[:, u : 2 * P : 2], ident[:])
+            copy(
+                out=y_words[ch][:].bitcast(F32).rearrange("p (n u) -> p n u", u=2),
+                in_=sig_banks[ch][:, 0 : 2 * P].rearrange("p (u n) -> p n u", u=2),
+            )
 
         def store_codes(h):
             for ch in range(2):
                 s0 = 256 * ch + P * h
                 nc.vector.quantize_mx(
-                    out=y_codes[h][:, P * ch : P * (ch + 1)].bitcast(FP8X4), scales=y_scales[:, s0 : s0 + P], in_=y_bf[ch][:]
+                    out=y_codes[h][:, P * ch : P * (ch + 1)].bitcast(FP8X4), scales=y_scales[:, s0 : s0 + P], in_=y_words[ch][:]
                 )
             nc.sync.dma_start(
                 out=out_1[:, :, P * h : P * (h + 1), :].rearrange("g p m t -> p g (m t)").bitcast(I32),
@@ -361,9 +355,6 @@ def tile_schnetfilterinteraction_x2_kernel(
                 for n, k in enumerate(first_last(c + 1)):
                     sig_at.setdefault(len(front) + SIG_START[c] + (n + SIG_LEAD) // SIG_RATE, []).append(k)
             front.extend(range(starts[c], starts[c + 1]))
-            if c < len(PAUSES):
-                front.extend([None] * PAUSES[c])
-        front.append(None)
         last_chunk = starts[-2]
 
         for k in first_last(0):
@@ -377,31 +368,37 @@ def tile_schnetfilterinteraction_x2_kernel(
         def at(s):
             return front[s] if s >= 0 else None
 
-        pool_cols = slice(0, POOL_COLS)
-        rest_cols = slice(POOL_COLS, 1024)
         added = 0
         made = 0
-        rows_due = -2
+        rows_due = -4
+        buf = 0
         for s in range(len(front)):
-            v, p, q = at(s), at(s - 1), at(s - 2)
+            v, p, q, m = at(s), at(s - 1), at(s - 2), at(s - 3)
             sig = sig_at.get(s, [])
-            if rows_due + 1 == s:
+            if rows_due + 2 == s:
                 store_codes(0)
             if q is not None:
-                if q < TILES - 2:
-                    f1_gain(q, nc.vector, rest_cols)
-                f1_quantize(q)
-            if p == TILES - 1:
-                f1_gain(p, nc.vector, slice(0, 1024))
-            elif p == TILES - 2:
-                f1_gain(p, nc.gpsimd, slice(0, 1024))
-            elif p is not None:
-                f1_gain(p, nc.gpsimd, pool_cols)
-            ending = p == TILES - 1
-            if ending:
-                for k in range(added, made):
+                f1_quantize(q, buf)
+            if p is not None:
+                f1_gain(p, buf)
+            if rows_due == s:
+                for ch in range(2):
+                    store_rows(0, ch)
+                for ch in range(2):
+                    round_rows(0, ch, nc.scalar.copy)
+            elif not sig and made - added >= ADD_RUN:
+                for k in range(added, added + ADD_RUN):
                     add_up(k)
-                added = made
+                added = added + ADD_RUN
+                if added == N:
+                    sums_out([nc.scalar.copy, nc.scalar.copy])
+                    rows_due = s + 1
+            if rows_due + 1 == s:
+                for ch in range(2):
+                    turn_words(ch, nc.scalar.copy)
+            if m is not None:
+                message(m)
+                made = m + 1
             if v is not None:
                 if v >= last_chunk and v + LN_AHEAD < TILES:
                     log_pass(v + LN_AHEAD)
@@ -414,40 +411,41 @@ def tile_schnetfilterinteraction_x2_kernel(
                 nxt = v + 2 if v + 1 in starts else v + 1
                 others.extend([(again, nxt, 0), (again, nxt, 1)])
             for n in range(max(len(halves), len(others))):
-                if n < len(others):
-                    others[n][0](*others[n][1:])
                 if n < len(halves):
                     sigmoid_half(*halves[n])
+                if n < len(others):
+                    others[n][0](*others[n][1:])
             if sig and sig[-1] in starts:
                 first = sig[-1]
                 last = first + LN_AHEAD if first == last_chunk else starts[starts.index(first) + 1]
                 for k in range(first, last):
                     log_pass(k)
-            if rows_due == s:
-                store_rows(0)
-            if ending:
-                f1_quantize(p)
-                for ch in range(2):
-                    second_matmul(p, ch)
-            flush = s == len(front) - 2
-            if not sig and not ending and (made - added >= ADD_RUN or flush) and rows_due != s:
-                stop = made if flush else added + ADD_RUN
-                for k in range(added, stop):
-                    add_up(k)
-                added = stop
-                if added == N:
-                    sums_out()
-                    rows_due = s + 1
-            if q is not None:
-                message(q)
-                made = q + 1
 
+        if rows_due + 2 >= len(front):
+            store_codes(0)
+        f1_quantize(TILES - 2, buf)
+        f1_gain(TILES - 1, buf)
+        for ch in range(2):
+            second_matmul(TILES - 2, ch)
+        for k in range(added, made):
+            add_up(k)
+        message(TILES - 3)
+        add_up(TILES - 3)
+        message(TILES - 2)
+        f1_quantize(TILES - 1, buf)
+        for ch in range(2):
+            second_matmul(TILES - 1, ch)
         add_up(TILES - 2)
         message(TILES - 1)
         add_up(TILES - 1)
-        last_sums_out()
+        sums_out([nc.scalar.copy, nc.vector.tensor_copy])
+        for ch in range(2):
+            store_rows(1, ch)
+        for ch in range(2):
+            round_rows(1, ch, nc.vector.tensor_copy)
+        for ch in range(2):
+            turn_words(ch, nc.vector.tensor_copy)
         store_codes(1)
-        store_rows(1)
         for q in range(4):
             nc.scalar.dma_start(
                 out=out_2[:, 4 * q : 4 * q + 4, :].rearrange("g r m -> r g m").bitcast(I32),

@@ -23,12 +23,12 @@ GAMMA = 10.0
 PERIOD = 10.0
 LN_FLOOR = 2.0**-40
 CHUNKS = (6, 6, 4)
-SIG_START = (2, 2)
+SIG_START = 3
 SIG_RATE = 2
-SIG_LEAD = 1
 PROD_BUFS = 6
-ADD_RUN = 2
+VECTOR_GAINS = 2
 LN_AHEAD = 2
+ADD_RUN = 2
 
 
 def tile_schnetfilterinteraction_x2_kernel(
@@ -51,7 +51,6 @@ def tile_schnetfilterinteraction_x2_kernel(
         filt_banks = [bank("filt0"), bank("filt1")]
         sum_banks = [bank("sum0"), bank("sum1")]
 
-        d_sb = sbuf("d_sb", 16, BF16)
         mu_sb = sbuf("mu_sb", 4, BF16)
         gr_sb = sbuf("gr_sb", 4, BF16)
         gf_sb = sbuf("gf_sb", 8, BF16)
@@ -82,7 +81,7 @@ def tile_schnetfilterinteraction_x2_kernel(
         r_bf = [sbuf("r_bf%d" % k, 512, BF16) for k in range(2)]
         r_codes = sbuf("r_codes", TILES * P, U32)
         r_scales = sbuf("r_scales", TILES * P, U8)
-        f1_bf = [sbuf("f1_bf%d" % k, 1024, BF16) for k in range(2)]
+        f1_bf = sbuf("f1_bf", 1536, BF16)
         f1_codes = [sbuf("f1_codes%d" % k, 256, U32) for k in range(2)]
         f1_scales = [sbuf("f1_scales%d" % k, 256, U8) for k in range(2)]
         prod = [[sbuf("prod%d_%d" % (k, ch), 512, F32) for ch in range(2)] for k in range(PROD_BUFS)]
@@ -95,8 +94,10 @@ def tile_schnetfilterinteraction_x2_kernel(
 
         out_rows = out_0.rearrange("b i c -> (b i) c")
 
+        d_sb = d_feat[:, 0:16]
+
         nc.sync.dma_start(
-            out=d_sb[:].rearrange("p (h j) -> p h j", h=2),
+            out=d_sb.rearrange("p (h j) -> p h j", h=2),
             in_=dist.rearrange("b i j -> (b i) j").rearrange("(h p) j -> p h j", h=2),
         )
         nc.sync.dma_start(out=mu_sb[:], in_=mu.rearrange("(p t) -> p t", t=4))
@@ -134,32 +135,30 @@ def tile_schnetfilterinteraction_x2_kernel(
             )
         make_identity(nc, ident_bf[:])
         make_identity(nc, ident[:])
-
-        nc.vector.tensor_scalar(out=turns[:], in0=d_sb[:], scalar1=1.0 / PERIOD, scalar2=None, op0=ALU.mult)
-        nc.vector.scalar_tensor_tensor(
-            out=d_red[:], in0=turns[:], scalar=-PERIOD, in1=d_sb[:], op0=ALU.mult, op1=ALU.add
-        )
-        nc.scalar.activation(out=sin_d[:], in_=d_red[:], func=ACT.Sin, scale=math.pi / PERIOD)
-
-        nc.vector.tensor_tensor(out=d_sq[:], in0=d_sb[:], in1=d_sb[:], op=ALU.mult)
-        nc.vector.tensor_tensor(out=mu_sq[:], in0=mu_sb[:], in1=mu_sb[:], op=ALU.mult)
-        nc.vector.tensor_copy(out=d_feat[:, 0:16], in_=d_sb[:])
-        nc.vector.tensor_copy(out=d_feat[:, 16:32], in_=d_sq[:])
-        mu_wide = mu_sb[:].unsqueeze(2).to_broadcast([P, 4, 16])
-        mu_sq_wide = mu_sq[:].unsqueeze(2).to_broadcast([P, 4, 16])
-        nc.vector.tensor_copy(out=mu_feat3[:, :, 48:64], in_=mu_sq_wide)
-        nc.vector.tensor_tensor(out=d_feat[:, 32:48], in0=d_sq[:], in1=d_feat[:, 16:32], op=ALU.subtract)
-        nc.vector.tensor_scalar(out=mu_feat3[:, :, 0:16], in0=mu_wide, scalar1=-2.0, scalar2=None, op0=ALU.mult)
-        nc.vector.tensor_tensor(out=mu_feat3[:, :, 64:80], in0=mu_sq_wide, in1=mu_feat3[:, :, 48:64], op=ALU.subtract)
         nc.vector.tensor_reduce(
             out=row_mask[:], in_=ident_bf[:].rearrange("p (k s) -> p s k", s=16), axis=AX.X, op=ALU.add
         )
+
+        nc.vector.tensor_scalar(out=turns[:], in0=d_sb, scalar1=1.0 / PERIOD, scalar2=None, op0=ALU.mult)
+        nc.vector.scalar_tensor_tensor(
+            out=d_red[:], in0=turns[:], scalar=-PERIOD, in1=d_sb, op0=ALU.mult, op1=ALU.add
+        )
+        nc.scalar.activation(out=sin_d[:], in_=d_red[:], func=ACT.Sin, scale=math.pi / PERIOD)
+
         d_t = filt_banks[0][:].bitcast(BF16)
         mu_t = filt_banks[1][:].bitcast(BF16)
-        nc.tensor.transpose(d_t[:, 0:P], d_feat[:], ident_bf[:])
+        mu_wide = mu_sb[:].unsqueeze(2).to_broadcast([P, 4, 16])
+        mu_sq_wide = mu_sq[:].unsqueeze(2).to_broadcast([P, 4, 16])
+        nc.vector.tensor_tensor(out=mu_sq[:], in0=mu_sb[:], in1=mu_sb[:], op=ALU.mult)
+        nc.vector.tensor_scalar(out=mu_feat3[:, :, 0:16], in0=mu_wide, scalar1=-2.0, scalar2=None, op0=ALU.mult)
+        nc.vector.tensor_copy(out=mu_feat3[:, :, 48:64], in_=mu_sq_wide)
+        nc.vector.tensor_tensor(out=d_sq[:], in0=d_sb, in1=d_sb, op=ALU.mult)
+        nc.vector.tensor_tensor(out=mu_feat3[:, :, 64:80], in0=mu_sq_wide, in1=mu_feat3[:, :, 48:64], op=ALU.subtract)
+        nc.vector.tensor_copy(out=d_feat[:, 16:32], in_=d_sq[:])
+        nc.vector.tensor_tensor(out=d_feat[:, 32:48], in0=d_sq[:], in1=d_feat[:, 16:32], op=ALU.subtract)
         for t in range(4):
             nc.tensor.transpose(mu_t[:, t * P : (t + 1) * P], mu_feat[:, t * P : (t + 1) * P], ident_bf[:])
-        nc.vector.tensor_scalar(out=neg_gr[:], in0=gr_sb[:], scalar1=-1.0, scalar2=None, op0=ALU.mult)
+        nc.tensor.transpose(d_t[:, 0:P], d_feat[:], ident_bf[:])
         nc.vector.tensor_copy(out=mu_rows[:], in_=mu_t[:, 0 : 4 * P])
         for k in range(TILES):
             nc.vector.tensor_scalar(
@@ -169,6 +168,7 @@ def tile_schnetfilterinteraction_x2_kernel(
                 scalar2=None,
                 op0=ALU.mult,
             )
+        nc.vector.tensor_scalar(out=neg_gr[:], in0=gr_sb[:], scalar1=-1.0, scalar2=None, op0=ALU.mult)
 
         def words_last(ap):
             return ap.rearrange("p (t n) -> p n t", t=4)
@@ -250,13 +250,19 @@ def tile_schnetfilterinteraction_x2_kernel(
                 )
 
         def sigmoid_half(k, g):
-            first_matmul(k, g, sig_banks[g])
+            c = max(n for n in range(len(CHUNKS)) if starts[n] <= k)
+            from_end = CHUNKS[c] - 1 - first_last(c).index(k)
+            banks = sum_banks if c < 2 and from_end % 2 else sig_banks
+            first_matmul(k, g, banks[g])
             nc.scalar.activation(
-                out=words(work[k][:, 512 * g : 512 * (g + 1)]), in_=words_last(sig_banks[g][:]), func=ACT.Sigmoid
+                out=words(work[k][:, 512 * g : 512 * (g + 1)]), in_=words_last(banks[g][:]), func=ACT.Sigmoid
             )
 
         def log_pass(k):
-            nc.scalar.activation(out=work[k][:], in_=work[k][:], func=ACT.Ln, scale=2.0, bias=LN_FLOOR)
+            width = 512 if k in starts else F
+            for c0 in range(0, F, width):
+                part = work[k][:, c0 : c0 + width]
+                nc.scalar.activation(out=part, in_=part, func=ACT.Ln, scale=2.0, bias=LN_FLOOR)
 
         def again(k, g):
             first_matmul(k, g, lin_banks[g])
@@ -269,11 +275,21 @@ def tile_schnetfilterinteraction_x2_kernel(
                     out=half, in0=words_last(src[g][:]), scalar=math.log(2.0), in1=half, op0=ALU.add, op1=ALU.min
                 )
 
-        def f1_gain(k, buf):
-            nc.gpsimd.tensor_tensor(out=f1_bf[buf][:], in0=work[k][:], in1=neg_gf[:], op=ALU.mult)
+        def f1_start(k):
+            return 0 if k % 2 else 512
 
-        def f1_quantize(k, buf):
-            nc.vector.quantize_mx(out=f1_codes[k % 2][:].bitcast(FP8X4), scales=f1_scales[k % 2][:], in_=f1_bf[buf][:])
+        def f1_gain(k):
+            engine = nc.vector if k < VECTOR_GAINS else nc.gpsimd
+            engine.tensor_tensor(out=f1_bf[:, f1_start(k) : f1_start(k) + F], in0=work[k][:], in1=neg_gf[:], op=ALU.mult)
+
+        def f1_quantize(k):
+            for g in (k % 2, 1 - k % 2):
+                c0 = f1_start(k) + 512 * g
+                nc.vector.quantize_mx(
+                    out=f1_codes[k % 2][:, P * g : P * (g + 1)].bitcast(FP8X4),
+                    scales=f1_scales[k % 2][:, P * g : P * (g + 1)],
+                    in_=f1_bf[:, c0 : c0 + 512],
+                )
 
         def second_matmul(k, ch):
             dst = (lin_banks if k == TILES - 2 else filt_banks)[ch]
@@ -301,9 +317,9 @@ def tile_schnetfilterinteraction_x2_kernel(
                     op1=ALU.mult,
                 )
 
-        def add_up(k):
+        def add_up(k, halves=(0, 1)):
             j = k % N
-            for ch in range(2):
+            for ch in halves:
                 for t in range(4):
                     nc.tensor.matmul(
                         sum_banks[ch][:, t * P : (t + 1) * P],
@@ -318,23 +334,22 @@ def tile_schnetfilterinteraction_x2_kernel(
             for ch in range(2):
                 copies[ch](out=y_t[ch][:], in_=sum_banks[ch][:])
 
-        def store_rows(h, ch):
+        def turn_rows(ch, banks):
             for t in range(4):
-                nc.tensor.transpose(sig_banks[ch][:, t * P : (t + 1) * P], y_t[ch][:, t * P : (t + 1) * P], ident[:])
+                nc.tensor.transpose(banks[ch][:, t * P : (t + 1) * P], y_t[ch][:, t * P : (t + 1) * P], ident[:])
+
+        def store_rows(h, ch):
             rows = y_sb[2 * h + ch]
             nc.scalar.copy(out=rows[:], in_=sig_banks[ch][:])
             nc.sync.dma_start(out=out_rows[P * h : P * (h + 1), 512 * ch : 512 * (ch + 1)], in_=rows[:])
 
-        def round_rows(h, ch, copy):
-            copy(out=y_bf[ch][:], in_=y_sb[2 * h + ch][:])
-
-        def turn_words(ch, copy):
+        def turn_words(ch, banks, copy):
             pairs = y_bf[ch][:].bitcast(F32)
             for u in range(2):
-                nc.tensor.transpose(sig_banks[ch][:, u * P : (u + 1) * P], pairs[:, u : 2 * P : 2], ident[:])
+                nc.tensor.transpose(banks[ch][:, u * P : (u + 1) * P], pairs[:, u : 2 * P : 2], ident[:])
             copy(
                 out=y_words[ch][:].bitcast(F32).rearrange("p (n u) -> p n u", u=2),
-                in_=sig_banks[ch][:, 0 : 2 * P].rearrange("p (u n) -> p n u", u=2),
+                in_=banks[ch][:, 0 : 2 * P].rearrange("p (u n) -> p n u", u=2),
             )
 
         def store_codes(h):
@@ -352,8 +367,10 @@ def tile_schnetfilterinteraction_x2_kernel(
         sig_at = {}
         for c in range(len(CHUNKS)):
             if c + 1 < len(CHUNKS):
+                early = 2 if c == 0 else 1
                 for n, k in enumerate(first_last(c + 1)):
-                    sig_at.setdefault(len(front) + SIG_START[c] + (n + SIG_LEAD) // SIG_RATE, []).append(k)
+                    step = len(front) + (0 if n < early else SIG_START + (n - early) // SIG_RATE)
+                    sig_at.setdefault(step, []).append(k)
             front.extend(range(starts[c], starts[c + 1]))
         last_chunk = starts[-2]
 
@@ -368,34 +385,31 @@ def tile_schnetfilterinteraction_x2_kernel(
         def at(s):
             return front[s] if s >= 0 else None
 
+        first_free = max(s for s in sig_at if s < CHUNKS[0])
         added = 0
         made = 0
         rows_due = -4
-        buf = 0
         for s in range(len(front)):
             v, p, q, m = at(s), at(s - 1), at(s - 2), at(s - 3)
             sig = sig_at.get(s, [])
-            if rows_due + 2 == s:
-                store_codes(0)
             if q is not None:
-                f1_quantize(q, buf)
+                f1_quantize(q)
             if p is not None:
-                f1_gain(p, buf)
+                f1_gain(p)
             if rows_due == s:
                 for ch in range(2):
+                    turn_rows(ch, sig_banks)
                     store_rows(0, ch)
-                for ch in range(2):
-                    round_rows(0, ch, nc.scalar.copy)
-            elif not sig and made - added >= ADD_RUN:
+            elif (v in starts or not sig) and s > first_free and made - added >= ADD_RUN:
                 for k in range(added, added + ADD_RUN):
                     add_up(k)
                 added = added + ADD_RUN
                 if added == N:
                     sums_out([nc.scalar.copy, nc.scalar.copy])
-                    rows_due = s + 1
-            if rows_due + 1 == s:
+                    rows_due = max(s, last_chunk) + 1
+            if v == TILES - 1:
                 for ch in range(2):
-                    turn_words(ch, nc.scalar.copy)
+                    nc.scalar.copy(out=y_bf[ch][:], in_=y_sb[ch][:])
             if m is not None:
                 message(m)
                 made = m + 1
@@ -421,30 +435,33 @@ def tile_schnetfilterinteraction_x2_kernel(
                 for k in range(first, last):
                     log_pass(k)
 
-        if rows_due + 2 >= len(front):
-            store_codes(0)
-        f1_quantize(TILES - 2, buf)
-        f1_gain(TILES - 1, buf)
-        for ch in range(2):
-            second_matmul(TILES - 2, ch)
+        f1_quantize(TILES - 2)
+        f1_gain(TILES - 1)
         for k in range(added, made):
             add_up(k)
+        for ch in range(2):
+            second_matmul(TILES - 2, ch)
+        for ch in range(2):
+            turn_words(ch, sig_banks, nc.scalar.copy)
         message(TILES - 3)
         add_up(TILES - 3)
         message(TILES - 2)
-        f1_quantize(TILES - 1, buf)
+        add_up(TILES - 2, (0,))
+        f1_quantize(TILES - 1)
         for ch in range(2):
             second_matmul(TILES - 1, ch)
-        add_up(TILES - 2)
+        store_codes(0)
+        add_up(TILES - 2, (1,))
         message(TILES - 1)
         add_up(TILES - 1)
         sums_out([nc.scalar.copy, nc.vector.tensor_copy])
         for ch in range(2):
+            turn_rows(ch, sig_banks)
+            turn_rows(ch, lin_banks)
             store_rows(1, ch)
+            nc.vector.tensor_copy(out=y_bf[ch][:], in_=lin_banks[ch][:])
         for ch in range(2):
-            round_rows(1, ch, nc.vector.tensor_copy)
-        for ch in range(2):
-            turn_words(ch, nc.vector.tensor_copy)
+            turn_words(ch, filt_banks, nc.scalar.copy)
         store_codes(1)
         for q in range(4):
             nc.scalar.dma_start(

@@ -11,24 +11,22 @@ U32 = mybir.dt.uint32
 U8 = mybir.dt.uint8
 FP8X4 = mybir.dt.float8_e4m3fn_x4
 FP4X4 = mybir.dt.float4_e2m1fn_x4
-ACT = mybir.ActivationFunctionType
 ALU = mybir.AluOpType
-AX = mybir.AxisListType
+ACT = mybir.ActivationFunctionType
+ENG = mybir.EngineType
 
-B, N, G, F, C = 32, 8, 512, 1024, 1024
-FLOPS = 2 * B * N * N * (G * F + F * C)
 P = 128
+ATOMS = 8
 TILES = 16
 GAMMA = 10.0
-PERIOD = 10.0
-LN_FLOOR = 2.0**-40
-CHUNKS = (6, 6, 4)
-SIG_START = 3
-SIG_RATE = 2
-PROD_BUFS = 6
-VECTOR_GAINS = 2
-LN_AHEAD = 2
-ADD_RUN = 2
+CUTOFF = 5.0
+LN2 = math.log(2.0)
+LN_FLOOR = 2.0 ** -63
+ORDER = [('q', 0), ('q', 1), ('E', 0), ('E', 1), ('q', 2), ('E', 2), ('q', 3), ('E', 3), ('q', 4), ('E', 4), ('q', 5), ('E', 5), ('q', 6), ('gr', 0), ('E', 6), ('q', 7), ('gr', 1), ('E', 7), ('q', 8), ('qr', 0), ('gr', 2), ('E', 8), ('q', 9), ('qr', 1), ('gr', 3), ('E', 9), ('q', 10), ('qr', 2), ('E', 10), ('q', 11), ('gr', 4), ('E', 11), ('q', 12), ('qr', 3), ('gr', 5), ('E', 12), ('q', 13), ('qr', 4), ('gr', 6), ('E', 13), ('q', 14), ('qr', 5), ('gr', 7), ('E', 14), ('q', 15), ('S', 0, 0), ('qr', 6), ('E', 15), ('gr', 8), ('S', 4, 0), ('S', 0, 1), ('qr', 7), ('S', 4, 1), ('gr', 9), ('S', 1, 0), ('qr', 8), ('S', 1, 1), ('gr', 10), ('S', 2, 0), ('qr', 9), ('S', 2, 1), ('gr', 11), ('sg', 4, 0), ('qr', 10), ('sg', 4, 1), ('S', 5, 0), ('gr', 12), ('sg', 5, 0), ('S', 5, 1), ('qr', 11), ('gr', 13), ('sg', 5, 1), ('S', 6, 0), ('qr', 12), ('gr', 14), ('sg', 6, 0), ('S', 6, 1), ('qr', 13), ('gr', 15), ('sg', 6, 1), ('S', 3, 0), ('qr', 14), ('sg', 0, 0), ('S', 3, 1), ('qr', 15), ('gfb',), ('sg', 0, 1), ('sg', 1, 0), ('sg', 1, 1), ('sg', 2, 0), ('sg', 2, 1), ('sg', 3, 0), ('sg', 3, 1), ('ln', 0), ('ln', 1), ('gd', 0, 0), ('gd', 0, 1), ('ln', 2), ('gn', 0), ('ln', 3), ('gd', 1, 0), ('gd', 1, 1), ('ln', 4), ('qf', 0), ('gd', 2, 0), ('F', 0, 0), ('gn', 1), ('gd', 2, 1), ('F', 0, 1), ('ln', 5), ('C', 0, 0), ('G', 4, 0), ('G', 4, 1), ('C', 0, 1), ('ln', 6), ('T', 0, 0), ('T', 0, 1), ('qf', 1), ('gd', 3, 0), ('F', 1, 0), ('gn', 2), ('gd', 3, 1), ('S', 8, 0), ('F', 1, 1), ('C', 1, 0), ('S', 8, 1), ('C', 1, 1), ('sg', 8, 0), ('T', 1, 0), ('sg', 8, 1), ('T', 1, 1), ('qf', 2), ('gd', 4, 0), ('S', 9, 0), ('gn', 3), ('S', 9, 1), ('sg', 9, 0), ('gd', 4, 1), ('F', 2, 0), ('sg', 9, 1), ('S', 10, 0), ('C', 2, 0), ('F', 2, 1), ('sg', 10, 0), ('S', 10, 1), ('C', 2, 1), ('S', 11, 0), ('sg', 10, 1), ('qf', 3), ('G', 5, 0), ('sg', 11, 0), ('G', 5, 1), ('gn', 4), ('gd', 5, 0), ('S', 11, 1), ('gd', 5, 1), ('S', 12, 0), ('sg', 11, 1), ('F', 3, 0), ('sg', 12, 0), ('S', 12, 1), ('C', 3, 0), ('F', 3, 1), ('sg', 12, 1), ('S', 7, 0), ('C', 3, 1), ('S', 7, 1), ('sg', 7, 0), ('qf', 4), ('G', 6, 0), ('sg', 7, 1), ('G', 6, 1), ('gn', 5), ('gd', 6, 0), ('F', 4, 0), ('gd', 6, 1), ('F', 4, 1), ('C', 4, 0), ('G', 8, 0), ('C', 4, 1), ('G', 8, 1), ('T', 2, 0), ('ln', 7), ('qf', 5), ('T', 2, 1), ('gn', 6), ('T', 3, 0), ('T', 3, 1), ('ln', 8), ('gd', 7, 0), ('T', 4, 0), ('T', 4, 1), ('gd', 7, 1), ('S', 14, 0), ('ln', 9), ('S', 14, 1), ('F', 5, 0), ('ln', 10), ('F', 5, 1), ('C', 5, 0), ('C', 5, 1), ('T', 5, 0), ('ln', 11), ('qf', 6), ('T', 5, 1), ('gd', 8, 0), ('gn', 7), ('F', 6, 0), ('gd', 8, 1), ('ln', 12), ('F', 6, 1), ('C', 6, 0), ('G', 9, 0), ('C', 6, 1), ('G', 9, 1), ('T', 6, 0), ('qf', 7), ('T', 6, 1), ('gd', 9, 0), ('F', 7, 0), ('gn', 8), ('gd', 9, 1), ('sg', 14, 0), ('F', 7, 1), ('C', 7, 0), ('sg', 14, 1), ('G', 10, 0), ('S', 15, 0), ('C', 7, 1), ('S', 15, 1), ('sg', 15, 0), ('G', 10, 1), ('qf', 8), ('sg', 15, 1), ('T', 7, 0), ('gd', 10, 0), ('gn', 9), ('T', 7, 1), ('gd', 10, 1), ('S', 13, 0), ('rt', 0, 0), ('S', 13, 1), ('sg', 13, 0), ('F', 8, 0), ('rt', 0, 1), ('sg', 13, 1), ('F', 8, 1), ('C', 8, 0), ('G', 11, 0), ('C', 8, 1), ('G', 11, 1), ('T', 8, 0), ('qf', 9), ('gd', 11, 0), ('T', 8, 1), ('gn', 10), ('F', 9, 0), ('ln', 13), ('gd', 11, 1), ('F', 9, 1), ('C', 9, 0), ('ln', 14), ('G', 12, 0), ('C', 9, 1), ('G', 12, 1), ('T', 9, 0), ('qf', 10), ('ln', 15), ('gd', 12, 0), ('T', 9, 1), ('gn', 11), ('F', 10, 0), ('gd', 12, 1), ('rb', 0, 0), ('F', 10, 1), ('C', 10, 0), ('G', 14, 0), ('C', 10, 1), ('G', 14, 1), ('T', 10, 0), ('qf', 11), ('T', 10, 1), ('gd', 13, 0), ('gn', 12), ('F', 11, 0), ('gd', 13, 1), ('F', 11, 1), ('C', 11, 0), ('B', 0, 0), ('C', 11, 1), ('T', 11, 0), ('ro', 0, 0), ('T', 11, 1), ('qf', 12), ('rb', 0, 1), ('B', 0, 1), ('gd', 14, 0), ('gn', 13), ('F', 12, 0), ('ro', 0, 1), ('gd', 14, 1), ('F', 12, 1), ('C', 12, 0), ('G', 15, 0), ('C', 12, 1), ('G', 15, 1), ('T', 12, 0), ('qf', 13), ('T', 12, 1), ('gd', 15, 0), ('gn', 14), ('F', 13, 0), ('gd', 15, 1), ('F', 13, 1), ('C', 13, 0), ('C', 13, 1), ('T', 13, 0), ('T', 13, 1), ('qf', 14), ('gn', 15), ('F', 14, 0), ('F', 14, 1), ('C', 14, 0), ('C', 14, 1), ('T', 14, 0), ('qf', 15), ('T', 14, 1), ('F', 15, 0), ('F', 15, 1), ('C', 15, 0), ('C', 15, 1), ('T', 15, 0), ('rt', 1, 0), ('T', 15, 1), ('rt', 1, 1), ('rb', 1, 0), ('B', 1, 0), ('ro', 1, 0), ('rb', 1, 1), ('B', 1, 1), ('qo', 0), ('ro', 1, 1), ('qo', 1)]
+HELD = {0: "filt", 1: "acc", 2: "grd"}
+VECTOR_GAIN = (0, 15)
+
+FLOPS = 2 * 2048 * 512 * 1024 + 2 * 2048 * 1024 * 1024
 
 
 def tile_schnetfilterinteraction_x2_kernel(
@@ -36,435 +34,285 @@ def tile_schnetfilterinteraction_x2_kernel(
 ):
     nc = tc.nc
     with ExitStack() as ctx:
-        sb = ctx.enter_context(tc.tile_pool(name="sb", bufs=1))
-        ps = ctx.enter_context(tc.psum_pool(name="ps", bufs=1))
-        ctx.enter_context(tc.manual_schedule())
+        keep = ctx.enter_context(tc.tile_pool(name="keep", bufs=1))
+        work = ctx.enter_context(tc.tile_pool(name="work", bufs=3))
+        psum = ctx.enter_context(tc.psum_pool(name="psum", bufs=2))
+        ctx.enter_context(tc.manual_schedule(engines={ENG.Activation, ENG.DVE, ENG.Pool, ENG.SP, ENG.PE}))
 
-        def sbuf(name, width, dtype):
-            return sb.tile([P, width], dtype, name=name, align_bytes=64)
+        ident_bf = keep.tile([P, P], BF16)
+        ident_f32 = keep.tile([P, P], F32)
+        make_identity(nc, ident_bf[:])
+        make_identity(nc, ident_f32[:])
 
-        def bank(name):
-            return ps.tile([P, 512], F32, name=name)
+        s1_raw = keep.tile([P, 1024], U8, align_bytes=64)
+        s2 = keep.tile([P, 2, 1024], U8, align_bytes=64)
+        d_feat = keep.tile([P, TILES * 8 + 120], BF16)
+        mu_feat = keep.tile([P, 4, P], BF16)
+        d_slots = d_feat[:, 0 : TILES * 8].rearrange("p (k f) -> p k f", f=8)
+        nc.vector.memset(s1_raw[:].bitcast(I32), 0)
+        nc.vector.memset(d_feat[:].bitcast(I32), 0)
+        nc.vector.memset(mu_feat[:].rearrange("p t n -> p (t n)").bitcast(I32), 0)
+        nc.vector.memset(s2[:].rearrange("p g n -> p (g n)").bitcast(I32), 0)
+        nc.vector.memset(d_slots[:, :, 3:5], 1.0)
+        nc.vector.memset(mu_feat[:, :, 1:3], 1.0)
 
-        sig_banks = [bank("sig0"), bank("sig1")]
-        lin_banks = [bank("lin0"), bank("lin1")]
-        filt_banks = [bank("filt0"), bank("filt1")]
-        sum_banks = [bank("sum0"), bank("sum1")]
-
-        mu_sb = sbuf("mu_sb", 4, BF16)
-        gr_sb = sbuf("gr_sb", 4, BF16)
-        gf_sb = sbuf("gf_sb", 8, BF16)
-        w1_raw = sbuf("w1_raw", 2048, U8)
-        w1s_raw = sbuf("w1s_raw", 1024, U8)
-        w1_sb = sbuf("w1_sb", 2048, U8)
-        w1s_sb = sbuf("w1s_sb", 1024, U8)
-        w2_sb = sbuf("w2_sb", 4096, U8)
-        w2s_sb = sbuf("w2s_sb", 2048, U8)
-        x_rep = [sbuf("x_rep%d" % q, 4096, BF16) for q in range(4)]
-        ident = sbuf("ident", P, F32)
-        ident_bf = sbuf("ident_bf", P, BF16)
-        row_mask = sbuf("row_mask", 16, F32)
-        d_feat = sbuf("d_feat", P, BF16)
-        mu_feat = sbuf("mu_feat", 4 * P, BF16)
-        mu_rows = sbuf("mu_rows", 4 * P, BF16)
-        d_rows = sbuf("d_rows", TILES * P, BF16)
-        d_sq = sbuf("d_sq", 16, F32)
-        mu_sq = sbuf("mu_sq", 4, F32)
-        turns = sbuf("turns", 16, I32)
-        d_red = sbuf("d_red", 16, F32)
-        sin_d = sbuf("sin_d", 16, F32)
-        sin_sq = sbuf("sin_sq", 16, F32)
-        fc = sbuf("fc", 16, F32)
-        neg_gr = sbuf("neg_gr", 4, F32)
-        neg_gf = sbuf("neg_gf", 1024, F32)
-        work = [sbuf("work%d" % k, 1024, F32) for k in range(TILES)]
-        r_bf = [sbuf("r_bf%d" % k, 512, BF16) for k in range(2)]
-        r_codes = sbuf("r_codes", TILES * P, U32)
-        r_scales = sbuf("r_scales", TILES * P, U8)
-        f1_bf = sbuf("f1_bf", 1536, BF16)
-        f1_codes = [sbuf("f1_codes%d" % k, 256, U32) for k in range(2)]
-        f1_scales = [sbuf("f1_scales%d" % k, 256, U8) for k in range(2)]
-        prod = [[sbuf("prod%d_%d" % (k, ch), 512, F32) for ch in range(2)] for k in range(PROD_BUFS)]
-        y_t = [sbuf("y_t%d" % k, 512, F32) for k in range(2)]
-        y_bf = [sbuf("y_bf%d" % k, 512, BF16) for k in range(2)]
-        y_words = [sbuf("y_words%d" % k, 512, BF16) for k in range(2)]
-        y_sb = [sbuf("y_sb%d" % k, 512, F32) for k in range(4)]
-        y_codes = [sbuf("y_codes%d" % k, 256, U32) for k in range(2)]
-        y_scales = sbuf("y_scales", 512, U8)
-
-        out_rows = out_0.rearrange("b i c -> (b i) c")
-
-        d_sb = d_feat[:, 0:16]
-
-        nc.sync.dma_start(
-            out=d_sb.rearrange("p (h j) -> p h j", h=2),
-            in_=dist.rearrange("b i j -> (b i) j").rearrange("(h p) j -> p h j", h=2),
-        )
+        d_sb = keep.tile([P, TILES], BF16)
+        mu_sb = keep.tile([P, 4], BF16)
+        gr_sb = keep.tile([P, 4], BF16)
+        gf_sb = keep.tile([P, 2, 4], BF16)
+        w1_raw = keep.tile([P, 2048], U8, align_bytes=64)
+        w2 = keep.tile([P, 2, 2048], U8, align_bytes=64)
+        x_sb = keep.tile([P, ATOMS, 1024], BF16)
+        nc.sync.dma_start(out=d_sb[:], in_=dist.rearrange("b i j -> (b i j)").rearrange("(p k) -> p k", k=TILES))
         nc.sync.dma_start(out=mu_sb[:], in_=mu.rearrange("(p t) -> p t", t=4))
         nc.sync.dma_start(out=gr_sb[:], in_=gr.rearrange("(p t) -> p t", t=4))
-        nc.sync.dma_start(out=w1_raw[:].bitcast(I32), in_=w1_words[0].bitcast(I32))
-        nc.vector.memset(w1s_raw[:].bitcast(I32), 0)
-        nc.vector.memset(d_feat[:, 48:80], 1.0)
-        nc.vector.memset(d_feat[:, 80:128], 0.0)
-        mu_feat3 = mu_feat[:].rearrange("p (t s) -> p t s", t=4)
-        nc.vector.memset(mu_feat3[:, :, 16:48], 1.0)
-        nc.vector.memset(mu_feat3[:, :, 80:128], 0.0)
-        nc.vector.memset(w2s_sb[:].bitcast(I32), 0)
         for q in range(4):
             nc.sync.dma_start(
-                out=w1s_raw[32 * q : 32 * q + 4, :].bitcast(I32), in_=w1_scales[0, 4 * q : 4 * q + 4, :].bitcast(I32)
+                out=s1_raw[32 * q : 32 * q + 4, :].bitcast(I32), in_=w1_scales[0, 4 * q : 4 * q + 4, :].bitcast(I32)
             )
-        nc.sync.dma_start(
-            out=gf_sb[:].rearrange("p (g t) -> p g t", g=2), in_=gf.rearrange("(g p t) -> p g t", g=2, t=4)
-        )
+        nc.sync.dma_start(out=w1_raw[:].bitcast(I32), in_=w1_words[0].bitcast(I32))
+        nc.sync.dma_start(out=gf_sb[:], in_=gf.rearrange("(g p t) -> p g t", g=2, t=4))
         for q in range(4):
             nc.sync.dma_start(
-                out=w2s_sb[32 * q : 32 * q + 4, :].rearrange("r (g n) -> r g n", g=2).bitcast(I32),
+                out=s2[32 * q : 32 * q + 4, :, :].bitcast(I32),
                 in_=w2_scales[:, 4 * q : 4 * q + 4, :].rearrange("g r n -> r g n").bitcast(I32),
             )
-        nc.sync.dma_start(
-            out=w2_sb[:].rearrange("p (g n) -> p g n", g=2).bitcast(I32),
-            in_=w2_words.rearrange("g p n -> p g n").bitcast(I32),
-        )
-        x_b = x.rearrange("b j c -> b (j c)")
-        for q in range(4):
-            h, jh = divmod(q, 2)
-            nc.sync.dma_start(
-                out=x_rep[q][:],
-                in_=x_b[16 * h : 16 * h + 16, 4096 * jh : 4096 * (jh + 1)].unsqueeze(1).to_broadcast([16, 8, 4096]),
-            )
-        make_identity(nc, ident_bf[:])
-        make_identity(nc, ident[:])
-        nc.vector.tensor_reduce(
-            out=row_mask[:], in_=ident_bf[:].rearrange("p (k s) -> p s k", s=16), axis=AX.X, op=ALU.add
-        )
+        nc.sync.dma_start(out=w2[:].bitcast(I32), in_=w2_words.rearrange("g p n -> p g n").bitcast(I32))
+        x_rows = x.rearrange("b j c -> b (j c)")
+        x_flat = x_sb[:].rearrange("p j c -> p (j c)")
+        for r in range(4):
+            nc.sync.dma_start(out=x_flat[r:P:4, :], in_=x_rows)
 
-        nc.vector.tensor_scalar(out=turns[:], in0=d_sb, scalar1=1.0 / PERIOD, scalar2=None, op0=ALU.mult)
+        turns_int = keep.tile([P, TILES], I32)
+        turns = keep.tile([P, TILES], F32)
+        sine = keep.tile([P, TILES], F32)
+        nc.vector.tensor_scalar(
+            out=turns_int[:], in0=d_sb[:], scalar1=0.5 / CUTOFF, scalar2=None, op0=ALU.mult
+        )
+        d_sq = keep.tile([P, TILES], F32)
+        mu_sq = keep.tile([P, 4], F32)
+        nc.vector.tensor_tensor(out=d_sq[:], in0=d_sb[:], in1=d_sb[:], op=ALU.mult)
         nc.vector.scalar_tensor_tensor(
-            out=d_red[:], in0=turns[:], scalar=-PERIOD, in1=d_sb, op0=ALU.mult, op1=ALU.add
+            out=turns[:], in0=d_sb[:], scalar=0.5 / CUTOFF, in1=turns_int[:], op0=ALU.mult, op1=ALU.subtract
         )
-        nc.scalar.activation(out=sin_d[:], in_=d_red[:], func=ACT.Sin, scale=math.pi / PERIOD)
+        nc.scalar.activation(out=sine[:], in_=turns[:], func=ACT.Sin, scale=math.pi)
 
-        d_t = filt_banks[0][:].bitcast(BF16)
-        mu_t = filt_banks[1][:].bitcast(BF16)
-        mu_wide = mu_sb[:].unsqueeze(2).to_broadcast([P, 4, 16])
-        mu_sq_wide = mu_sq[:].unsqueeze(2).to_broadcast([P, 4, 16])
         nc.vector.tensor_tensor(out=mu_sq[:], in0=mu_sb[:], in1=mu_sb[:], op=ALU.mult)
-        nc.vector.tensor_scalar(out=mu_feat3[:, :, 0:16], in0=mu_wide, scalar1=-2.0, scalar2=None, op0=ALU.mult)
-        nc.vector.tensor_copy(out=mu_feat3[:, :, 48:64], in_=mu_sq_wide)
-        nc.vector.tensor_tensor(out=d_sq[:], in0=d_sb, in1=d_sb, op=ALU.mult)
-        nc.vector.tensor_tensor(out=mu_feat3[:, :, 64:80], in0=mu_sq_wide, in1=mu_feat3[:, :, 48:64], op=ALU.subtract)
-        nc.vector.tensor_copy(out=d_feat[:, 16:32], in_=d_sq[:])
-        nc.vector.tensor_tensor(out=d_feat[:, 32:48], in0=d_sq[:], in1=d_feat[:, 16:32], op=ALU.subtract)
+        nc.vector.tensor_copy(out=d_slots[:, :, 1], in_=d_sq[:])
+        nc.vector.tensor_copy(out=mu_feat[:, :, 3], in_=mu_sq[:])
+        nc.vector.tensor_copy(out=d_slots[:, :, 0], in_=d_sb[:])
+        nc.vector.tensor_scalar(out=mu_feat[:, :, 0], in0=mu_sb[:], scalar1=-2.0, scalar2=None, op0=ALU.mult)
+        nc.vector.tensor_tensor(out=mu_feat[:, :, 4], in0=mu_sq[:], in1=mu_feat[:, :, 3], op=ALU.subtract)
+        nc.vector.tensor_tensor(out=d_slots[:, :, 2], in0=d_sq[:], in1=d_slots[:, :, 1], op=ALU.subtract)
+
+        mu_rows = keep.tile([P, 4, P], BF16)
+        d_rows = keep.tile([P, TILES, P], BF16)
+        turned = psum.tile([P, 4, P], BF16, tag="grd", name="turned_mu")
         for t in range(4):
-            nc.tensor.transpose(mu_t[:, t * P : (t + 1) * P], mu_feat[:, t * P : (t + 1) * P], ident_bf[:])
-        nc.tensor.transpose(d_t[:, 0:P], d_feat[:], ident_bf[:])
-        nc.vector.tensor_copy(out=mu_rows[:], in_=mu_t[:, 0 : 4 * P])
-        for k in range(TILES):
-            nc.vector.tensor_scalar(
-                out=d_rows[:, k * P : (k + 1) * P],
-                in0=d_t[:, 0:P],
-                scalar1=row_mask[:, k : k + 1],
-                scalar2=None,
-                op0=ALU.mult,
-            )
-        nc.vector.tensor_scalar(out=neg_gr[:], in0=gr_sb[:], scalar1=-1.0, scalar2=None, op0=ALU.mult)
+            nc.tensor.transpose(turned[:, t, :], mu_feat[:, t, :], ident_bf[:])
+        nc.vector.tensor_copy(out=mu_rows[:], in_=turned[:])
+        r_codes = keep.tile([P, TILES, P], U32, align_bytes=64)
+        r_scales = keep.tile([P, TILES, P], U8, align_bytes=64)
+        fc = keep.tile([P, TILES], F32)
+        sine_sq = keep.tile([P, TILES], F32)
+        neg_gf = keep.tile([P, 2, P, 4], BF16)
+        plane_bf = keep.tile([P, 2, 2 * P, 4], BF16, align_bytes=64)
+        codes = keep.tile([P, 2, 2 * P], U32, align_bytes=64)
+        scales = keep.tile([P, 2, 2 * P], U8, align_bytes=64)
+        out_rows = out_0.rearrange("b i c -> (b i) c").rearrange("(q h) c -> q h c", h=2)
+        tl = {}
 
-        def words_last(ap):
-            return ap.rearrange("p (t n) -> p n t", t=4)
-
-        def words(ap):
-            return ap.rearrange("p (n t) -> p n t", t=4)
-
-        gauss_banks = sig_banks + lin_banks
-        for k in range(TILES):
-            sq = gauss_banks[k % 4]
+        def neg_h(k, g, tag):
+            bank = psum.tile([P, 4, P], F32, tag=tag, name="neg_h")
             for t in range(4):
-                nc.tensor.matmul(
-                    sq[:, t * P : (t + 1) * P],
-                    lhsT=mu_rows[:, t * P : (t + 1) * P],
-                    rhs=d_rows[:, k * P : (k + 1) * P],
-                    start=True,
-                    stop=True,
-                )
-            nc.scalar.activation(out=words(work[k][:, 0:512]), in_=words_last(sq[:]), func=ACT.Exp, scale=-GAMMA)
-
-        def r_gain(k):
-            nc.vector.tensor_tensor(
-                out=words(r_bf[k % 2][:]),
-                in0=words(work[k][:, 0:512]),
-                in1=neg_gr[:].unsqueeze(1).to_broadcast([P, P, 4]),
-                op=ALU.mult,
-            )
-
-        def r_quantize(k):
-            cols = slice(k * P, (k + 1) * P)
-            nc.vector.quantize_mx(out=r_codes[:, cols].bitcast(FP8X4), scales=r_scales[:, cols], in_=r_bf[k % 2][:])
-
-        def r_tiles(first, last):
-            r_gain(first)
-            for k in range(first, last):
-                if k + 1 < last:
-                    r_gain(k + 1)
-                r_quantize(k)
-
-        nc.vector.tensor_copy(
-            out=w1_sb[:].rearrange("p (g t m b) -> p g t m b", g=2, t=4, b=2),
-            in_=w1_raw[:].rearrange("p (g m t b) -> p g t m b", g=2, t=4, b=2),
-        )
-        r_tiles(0, CHUNKS[0])
-        nc.vector.tensor_copy(
-            out=w1s_sb[:].rearrange("p (g t m) -> p g t m", g=2, t=4),
-            in_=w1s_raw[:].rearrange("p (g m t) -> p g t m", g=2, t=4),
-        )
-        nc.vector.tensor_tensor(out=sin_sq[:], in0=sin_d[:], in1=sin_d[:], op=ALU.mult)
-        nc.vector.tensor_scalar(
-            out=neg_gf[:].rearrange("p (g n t) -> p g n t", g=2, t=4),
-            in0=gf_sb[:].rearrange("p (g t) -> p g t", g=2).unsqueeze(2).to_broadcast([P, 2, P, 4]),
-            scalar1=-1.0,
-            scalar2=None,
-            op0=ALU.mult,
-        )
-        nc.vector.tensor_scalar(
-            out=fc[:], in0=sin_sq[:], scalar1=-1.0 / math.sqrt(N), scalar2=1.0 / math.sqrt(N), op0=ALU.mult, op1=ALU.add
-        )
-        r_tiles(CHUNKS[0], TILES)
-
-        starts = [sum(CHUNKS[:c]) for c in range(len(CHUNKS) + 1)]
-
-        def first_last(c):
-            return list(range(starts[c] + 1, starts[c + 1])) + [starts[c]]
-
-        def first_matmul(k, g, dst):
-            cols = slice(k * P, (k + 1) * P)
-            for t in range(4):
-                s = 4 * g + t
                 nc.tensor.matmul_mx(
-                    out=dst[:, t * P : (t + 1) * P],
-                    lhsT=w1_sb[:, 2 * P * s : 2 * P * (s + 1)].bitcast(FP4X4),
-                    lhsT_scale=w1s_sb[:, P * s : P * (s + 1)],
-                    rhs=r_codes[:, cols].bitcast(FP8X4),
-                    rhs_scale=r_scales[:, cols],
+                    out=bank[:, t, :],
+                    lhsT=w1[:, g, t, :].bitcast(FP4X4),
+                    lhsT_scale=s1[:, g, t, :],
+                    rhs=r_codes[:, k, :].bitcast(FP8X4),
+                    rhs_scale=r_scales[:, k, :],
                     start=True,
                     stop=True,
                 )
+            tl["h", k, g] = bank[:].rearrange("p t n -> p n t")
 
-        def sigmoid_half(k, g):
-            c = max(n for n in range(len(CHUNKS)) if starts[n] <= k)
-            from_end = CHUNKS[c] - 1 - first_last(c).index(k)
-            banks = sum_banks if c < 2 and from_end % 2 else sig_banks
-            first_matmul(k, g, banks[g])
-            nc.scalar.activation(
-                out=words(work[k][:, 512 * g : 512 * (g + 1)]), in_=words_last(banks[g][:]), func=ACT.Sigmoid
-            )
-
-        def log_pass(k):
-            width = 512 if k in starts else F
-            for c0 in range(0, F, width):
-                part = work[k][:, c0 : c0 + width]
-                nc.scalar.activation(out=part, in_=part, func=ACT.Ln, scale=2.0, bias=LN_FLOOR)
-
-        def again(k, g):
-            first_matmul(k, g, lin_banks[g])
-
-        def guard(k):
-            src = sig_banks if k in starts else lin_banks
-            for g in range(2):
-                half = words(work[k][:, 512 * g : 512 * (g + 1)])
-                nc.vector.scalar_tensor_tensor(
-                    out=half, in0=words_last(src[g][:]), scalar=math.log(2.0), in1=half, op0=ALU.add, op1=ALU.min
+        def emit(step, k=0, g=0):
+            if step == "q":
+                sq = psum.tile([P, 4, P], F32, tag="sig", name="sq")
+                for t in range(4):
+                    nc.tensor.matmul(sq[:, t, :], lhsT=mu_rows[:, t, :], rhs=d_rows[:, k, :], start=True, stop=True)
+                tl["sq", k] = sq
+            elif step == "E":
+                rbf = work.tile([P, P, 4], F32, tag="rbf", bufs=TILES)
+                nc.scalar.activation(
+                    out=rbf[:], in_=tl["sq", k][:].rearrange("p t n -> p n t"), func=ACT.Exp, scale=-GAMMA
                 )
-
-        def f1_start(k):
-            return 0 if k % 2 else 512
-
-        def f1_gain(k):
-            engine = nc.vector if k < VECTOR_GAINS else nc.gpsimd
-            engine.tensor_tensor(out=f1_bf[:, f1_start(k) : f1_start(k) + F], in0=work[k][:], in1=neg_gf[:], op=ALU.mult)
-
-        def f1_quantize(k):
-            for g in (k % 2, 1 - k % 2):
-                c0 = f1_start(k) + 512 * g
+                tl["rbf", k] = rbf
+            elif step == "gr":
+                r_bf = work.tile([P, 4 * P], BF16, tag="r_bf", align_bytes=64)
+                nc.vector.tensor_tensor(
+                    out=r_bf[:].rearrange("p (n t) -> p n t", t=4),
+                    in0=tl["rbf", k][:],
+                    in1=neg_gr[:].unsqueeze(1).to_broadcast([P, P, 4]),
+                    op=ALU.mult,
+                )
+                tl["r_bf", k] = r_bf
+                if k == TILES - 1:
+                    nc.vector.tensor_tensor(out=sine_sq[:], in0=sine[:], in1=sine[:], op=ALU.mult)
+            elif step == "qr":
                 nc.vector.quantize_mx(
-                    out=f1_codes[k % 2][:, P * g : P * (g + 1)].bitcast(FP8X4),
-                    scales=f1_scales[k % 2][:, P * g : P * (g + 1)],
-                    in_=f1_bf[:, c0 : c0 + 512],
+                    out=r_codes[:, k, :].bitcast(FP8X4), scales=r_scales[:, k, :], in_=tl["r_bf", k][:]
                 )
-
-        def second_matmul(k, ch):
-            dst = (lin_banks if k == TILES - 2 else filt_banks)[ch]
-            for g in range(2):
-                nc.tensor.matmul_mx(
-                    out=dst[:],
-                    lhsT=f1_codes[k % 2][:, P * g : P * (g + 1)].bitcast(FP8X4),
-                    lhsT_scale=f1_scales[k % 2][:, P * g : P * (g + 1)],
-                    rhs=w2_sb[:, 2048 * g + 1024 * ch : 2048 * g + 1024 * (ch + 1)].bitcast(FP4X4),
-                    rhs_scale=w2s_sb[:, 1024 * g + 512 * ch : 1024 * g + 512 * (ch + 1)],
-                    start=(g == 0),
-                    stop=(g == 1),
+            elif step == "gfb":
+                inv_root = 1.0 / math.sqrt(ATOMS)
+                nc.vector.tensor_scalar(
+                    out=fc[:], in0=sine_sq[:], scalar1=-inv_root, scalar2=inv_root, op0=ALU.mult, op1=ALU.add
                 )
-
-        def message(k):
-            src = lin_banks if k == TILES - 2 else filt_banks
-            for ch in range(2):
-                x0 = 1024 * (k % 4) + 512 * ch
+                for u in range(2):
+                    nc.vector.tensor_scalar(
+                        out=neg_gf[:, u],
+                        in0=gf_sb[:, u, :].unsqueeze(1).to_broadcast([P, P, 4]),
+                        scalar1=-1.0,
+                        scalar2=None,
+                        op0=ALU.mult,
+                    )
+            elif step == "S":
+                neg_h(k, g, HELD.get(k, "sig"))
+            elif step == "G":
+                neg_h(k, g, "grd")
+            elif step == "sg":
+                if g == 0:
+                    tl["logs", k] = work.tile([P, 2, P, 4], F32, tag="logs", name="logs", bufs=TILES)
+                nc.scalar.activation(out=tl["logs", k][:, g], in_=tl["h", k, g], func=ACT.Sigmoid)
+            elif step == "ln":
+                flat = tl["logs", k][:].rearrange("p g n t -> p (g n t)")
+                nc.scalar.activation(out=flat, in_=flat, func=ACT.Ln, scale=2.0, bias=LN_FLOOR)
+            elif step == "gd":
+                if g == 0:
+                    tl["m", k] = work.tile([P, 2, P, 4], F32, tag="neg_ssp", name="neg_ssp")
                 nc.vector.scalar_tensor_tensor(
-                    out=prod[k % PROD_BUFS][ch][:],
-                    in0=src[ch][:],
+                    out=tl["m", k][:, g],
+                    in0=tl["h", k, g],
+                    scalar=LN2,
+                    in1=tl["logs", k][:, g],
+                    op0=ALU.add,
+                    op1=ALU.min,
+                )
+            elif step == "gn":
+                f_bf = work.tile([P, 1024], BF16, tag="f_bf", bufs=1, align_bytes=64)
+                engine = nc.vector if k in VECTOR_GAIN else nc.gpsimd
+                engine.tensor_tensor(
+                    out=f_bf[:],
+                    in0=tl["m", k][:].rearrange("p g n t -> p (g n t)"),
+                    in1=neg_gf[:].rearrange("p g n t -> p (g n t)"),
+                    op=ALU.mult,
+                )
+                tl["f_bf", k] = f_bf
+            elif step == "qf":
+                f_codes = work.tile([P, 2, P], U32, tag="f_codes", align_bytes=64)
+                f_scales = work.tile([P, 2, P], U8, tag="f_scales", align_bytes=64)
+                nc.vector.quantize_mx(
+                    out=f_codes[:].rearrange("p g n -> p (g n)").bitcast(FP8X4),
+                    scales=f_scales[:].rearrange("p g n -> p (g n)"),
+                    in_=tl["f_bf", k][:],
+                )
+                tl["fq", k] = (f_codes, f_scales)
+            elif step == "F":
+                filt = psum.tile([P, 512], F32, tag="filt")
+                f_codes, f_scales = tl["fq", k]
+                for u in range(2):
+                    nc.tensor.matmul_mx(
+                        out=filt[:],
+                        lhsT=f_codes[:, u, :].bitcast(FP8X4),
+                        lhsT_scale=f_scales[:, u, :],
+                        rhs=w2[:, u, 1024 * g : 1024 * (g + 1)].bitcast(FP4X4),
+                        rhs_scale=s2[:, u, 512 * g : 512 * (g + 1)],
+                        start=(u == 0),
+                        stop=(u == 1),
+                    )
+                tl["filt", k, g] = filt
+            elif step == "C":
+                msg = work.tile([P, 4, P], F32, tag="msg", bufs=6)
+                nc.vector.scalar_tensor_tensor(
+                    out=msg[:],
+                    in0=tl["filt", k, g][:].rearrange("q (p t) -> q t p", t=4),
                     scalar=fc[:, k : k + 1],
-                    in1=x_rep[k // 4][:, x0 : x0 + 512],
+                    in1=x_sb[:, k % ATOMS, 512 * g : 512 * (g + 1)].rearrange("q (p t) -> q t p", t=4),
                     op0=ALU.mult,
                     op1=ALU.mult,
                 )
-
-        def add_up(k, halves=(0, 1)):
-            j = k % N
-            for ch in halves:
+                tl["msg", k, g] = msg
+            elif step == "T":
+                h, j = divmod(k, ATOMS)
+                if j == 0:
+                    tl["acc", h, g] = psum.tile([P, 4, P], F32, tag="acc", name="acc")
                 for t in range(4):
                     nc.tensor.matmul(
-                        sum_banks[ch][:, t * P : (t + 1) * P],
-                        lhsT=prod[k % PROD_BUFS][ch][:, P * t : P * (t + 1)],
-                        rhs=ident[:],
+                        tl["acc", h, g][:, t, :],
+                        lhsT=tl["msg", k, g][:, t, :],
+                        rhs=ident_f32[:],
                         is_transpose=True,
                         start=(j == 0 and t == 0),
-                        stop=(j == N - 1 and t == 3),
+                        stop=(j == ATOMS - 1 and t == 3),
                     )
-
-        def sums_out(copies):
-            for ch in range(2):
-                copies[ch](out=y_t[ch][:], in_=sum_banks[ch][:])
-
-        def turn_rows(ch, banks):
-            for t in range(4):
-                nc.tensor.transpose(banks[ch][:, t * P : (t + 1) * P], y_t[ch][:, t * P : (t + 1) * P], ident[:])
-
-        def store_rows(h, ch):
-            rows = y_sb[2 * h + ch]
-            nc.scalar.copy(out=rows[:], in_=sig_banks[ch][:])
-            nc.sync.dma_start(out=out_rows[P * h : P * (h + 1), 512 * ch : 512 * (ch + 1)], in_=rows[:])
-
-        def turn_words(ch, banks, copy):
-            pairs = y_bf[ch][:].bitcast(F32)
-            for u in range(2):
-                nc.tensor.transpose(banks[ch][:, u * P : (u + 1) * P], pairs[:, u : 2 * P : 2], ident[:])
-            copy(
-                out=y_words[ch][:].bitcast(F32).rearrange("p (n u) -> p n u", u=2),
-                in_=banks[ch][:, 0 : 2 * P].rearrange("p (u n) -> p n u", u=2),
-            )
-
-        def store_codes(h):
-            for ch in range(2):
-                s0 = 256 * ch + P * h
-                nc.vector.quantize_mx(
-                    out=y_codes[h][:, P * ch : P * (ch + 1)].bitcast(FP8X4), scales=y_scales[:, s0 : s0 + P], in_=y_words[ch][:]
+            elif step == "rt":
+                tl["sums", k, g] = keep.tile([P, 4, P], F32, name="sums_%d_%d" % (k, g))
+                move = nc.scalar.copy if k == 1 else nc.vector.tensor_copy
+                move(out=tl["sums", k, g][:], in_=tl["acc", k, g][:])
+            elif step == "rb":
+                move = nc.scalar.copy if k == 0 else nc.vector.tensor_copy
+                move(
+                    out=plane_bf[:, g].rearrange("p (q h) t -> p q h t", h=2)[:, :, k, :],
+                    in_=tl["sums", k, g][:].rearrange("p t q -> p q t"),
                 )
-            nc.sync.dma_start(
-                out=out_1[:, :, P * h : P * (h + 1), :].rearrange("g p m t -> p g (m t)").bitcast(I32),
-                in_=y_codes[h][:].rearrange("p (g m) -> p g m", g=2).bitcast(I32),
-            )
+            elif step == "B":
+                back = psum.tile([P, 4, P], F32, tag="sig")
+                for t in range(4):
+                    nc.tensor.transpose(back[:, t, :], tl["sums", k, g][:, t, :], ident_f32[:])
+                tl["back", k, g] = back
+            elif step == "ro":
+                rows = work.tile([P, P, 4], F32, tag="rows", bufs=4)
+                nc.scalar.copy(out=rows[:], in_=tl["back", k, g][:].rearrange("q t p -> q p t"))
+                nc.sync.dma_start(
+                    out=out_rows[:, k, 512 * g : 512 * (g + 1)], in_=rows[:].rearrange("q p t -> q (p t)")
+                )
+            elif step == "qo":
+                nc.vector.quantize_mx(
+                    out=codes[:, k, :].bitcast(FP8X4),
+                    scales=scales[:, k, :],
+                    in_=plane_bf[:, k].rearrange("p m t -> p (m t)"),
+                )
+                nc.sync.dma_start(
+                    out=out_1[k].rearrange("p m t -> p (m t)").bitcast(I32), in_=codes[:, k, :].bitcast(I32)
+                )
 
-        front = []
-        sig_at = {}
-        for c in range(len(CHUNKS)):
-            if c + 1 < len(CHUNKS):
-                early = 2 if c == 0 else 1
-                for n, k in enumerate(first_last(c + 1)):
-                    step = len(front) + (0 if n < early else SIG_START + (n - early) // SIG_RATE)
-                    sig_at.setdefault(step, []).append(k)
-            front.extend(range(starts[c], starts[c + 1]))
-        last_chunk = starts[-2]
+        for c, tag in enumerate(("filt", "filt", "acc", "acc")):
+            turned = psum.tile([P, 4, P], BF16, tag=tag, name="turned_d")
+            for u in range(4):
+                k = 4 * c + u
+                nc.tensor.transpose(turned[:, u, :], d_feat[:, 8 * k : 8 * k + P], ident_bf[:])
+            nc.vector.tensor_copy(out=d_rows[:, 4 * c : 4 * c + 4, :], in_=turned[:])
+            if c == 0:
+                emit("q", 0)
+                emit("q", 1)
 
-        for k in first_last(0):
-            for g in range(2):
-                sigmoid_half(k, g)
+        neg_gr = keep.tile([P, 4], F32)
+        nc.vector.tensor_scalar(out=neg_gr[:], in0=gr_sb[:], scalar1=-1.0, scalar2=None, op0=ALU.mult)
+
+        w1 = keep.tile([P, 2, 4, 256], U8, align_bytes=64)
+        s1 = keep.tile([P, 2, 4, P], U8, align_bytes=64)
         for g in range(2):
-            again(1, g)
-        for k in range(CHUNKS[0]):
-            log_pass(k)
+            nc.vector.tensor_copy(
+                out=w1[:, g].rearrange("p t (m e) -> p t m e", e=2),
+                in_=w1_raw[:, 1024 * g : 1024 * (g + 1)].rearrange("p (m t e) -> p t m e", t=4, e=2),
+            )
+        nc.vector.tensor_copy(out=s1[:], in_=s1_raw[:].rearrange("p (g m t) -> p g t m", g=2, t=4))
 
-        def at(s):
-            return front[s] if s >= 0 else None
 
-        first_free = max(s for s in sig_at if s < CHUNKS[0])
-        added = 0
-        made = 0
-        rows_due = -4
-        for s in range(len(front)):
-            v, p, q, m = at(s), at(s - 1), at(s - 2), at(s - 3)
-            sig = sig_at.get(s, [])
-            if q is not None:
-                f1_quantize(q)
-            if p is not None:
-                f1_gain(p)
-            if rows_due == s:
-                for ch in range(2):
-                    turn_rows(ch, sig_banks)
-                    store_rows(0, ch)
-            elif (v in starts or not sig) and s > first_free and made - added >= ADD_RUN:
-                for k in range(added, added + ADD_RUN):
-                    add_up(k)
-                added = added + ADD_RUN
-                if added == N:
-                    sums_out([nc.scalar.copy, nc.scalar.copy])
-                    rows_due = max(s, last_chunk) + 1
-            if v == TILES - 1:
-                for ch in range(2):
-                    nc.scalar.copy(out=y_bf[ch][:], in_=y_sb[ch][:])
-            if m is not None:
-                message(m)
-                made = m + 1
-            if v is not None:
-                if v >= last_chunk and v + LN_AHEAD < TILES:
-                    log_pass(v + LN_AHEAD)
-                guard(v)
-            halves = [(k, g) for k in sig for g in range(2)]
-            others = []
-            if q is not None:
-                others.extend([(second_matmul, q, 0), (second_matmul, q, 1)])
-            if v is not None and v not in starts and v + 1 < TILES:
-                nxt = v + 2 if v + 1 in starts else v + 1
-                others.extend([(again, nxt, 0), (again, nxt, 1)])
-            for n in range(max(len(halves), len(others))):
-                if n < len(halves):
-                    sigmoid_half(*halves[n])
-                if n < len(others):
-                    others[n][0](*others[n][1:])
-            if sig and sig[-1] in starts:
-                first = sig[-1]
-                last = first + LN_AHEAD if first == last_chunk else starts[starts.index(first) + 1]
-                for k in range(first, last):
-                    log_pass(k)
-
-        f1_quantize(TILES - 2)
-        f1_gain(TILES - 1)
-        for k in range(added, made):
-            add_up(k)
-        for ch in range(2):
-            second_matmul(TILES - 2, ch)
-        for ch in range(2):
-            turn_words(ch, sig_banks, nc.scalar.copy)
-        message(TILES - 3)
-        add_up(TILES - 3)
-        message(TILES - 2)
-        add_up(TILES - 2, (0,))
-        f1_quantize(TILES - 1)
-        for ch in range(2):
-            second_matmul(TILES - 1, ch)
-        store_codes(0)
-        add_up(TILES - 2, (1,))
-        message(TILES - 1)
-        add_up(TILES - 1)
-        sums_out([nc.scalar.copy, nc.vector.tensor_copy])
-        for ch in range(2):
-            turn_rows(ch, sig_banks)
-            turn_rows(ch, lin_banks)
-            store_rows(1, ch)
-            nc.vector.tensor_copy(out=y_bf[ch][:], in_=lin_banks[ch][:])
-        for ch in range(2):
-            turn_words(ch, filt_banks, nc.scalar.copy)
-        store_codes(1)
+        for item in ORDER[2:]:
+            emit(*item)
         for q in range(4):
-            nc.scalar.dma_start(
+            nc.sync.dma_start(
                 out=out_2[:, 4 * q : 4 * q + 4, :].rearrange("g r m -> r g m").bitcast(I32),
-                in_=y_scales[32 * q : 32 * q + 4, :].rearrange("r (g m) -> r g m", g=2).bitcast(I32),
+                in_=scales[32 * q : 32 * q + 4, :, :].bitcast(I32),
             )

import math
from contextlib import ExitStack

import concourse.mybir as mybir
from concourse.masks import make_identity

F32 = mybir.dt.float32
BF16 = mybir.dt.bfloat16
I32 = mybir.dt.int32
U32 = mybir.dt.uint32
U8 = mybir.dt.uint8
FP8X4 = mybir.dt.float8_e4m3fn_x4
FP4X4 = mybir.dt.float4_e2m1fn_x4
ALU = mybir.AluOpType
ACT = mybir.ActivationFunctionType
ENG = mybir.EngineType

P = 128
ATOMS = 8
TILES = 16
GAMMA = 10.0
CUTOFF = 5.0
LN2 = math.log(2.0)
LN_FLOOR = 2.0 ** -63
ORDER = [('q', 0), ('q', 1), ('E', 0), ('E', 1), ('q', 2), ('E', 2), ('q', 3), ('E', 3), ('q', 4), ('E', 4), ('q', 5), ('E', 5), ('q', 6), ('gr', 0), ('E', 6), ('q', 7), ('gr', 1), ('E', 7), ('q', 8), ('qr', 0), ('gr', 2), ('E', 8), ('q', 9), ('qr', 1), ('gr', 3), ('E', 9), ('q', 10), ('qr', 2), ('E', 10), ('q', 11), ('gr', 4), ('E', 11), ('q', 12), ('qr', 3), ('gr', 5), ('E', 12), ('q', 13), ('qr', 4), ('gr', 6), ('E', 13), ('q', 14), ('qr', 5), ('gr', 7), ('E', 14), ('q', 15), ('S', 0, 0), ('qr', 6), ('E', 15), ('gr', 8), ('S', 4, 0), ('S', 0, 1), ('qr', 7), ('S', 4, 1), ('gr', 9), ('S', 1, 0), ('qr', 8), ('S', 1, 1), ('gr', 10), ('S', 2, 0), ('qr', 9), ('S', 2, 1), ('gr', 11), ('sg', 4, 0), ('qr', 10), ('sg', 4, 1), ('S', 5, 0), ('gr', 12), ('sg', 5, 0), ('S', 5, 1), ('qr', 11), ('gr', 13), ('sg', 5, 1), ('S', 6, 0), ('qr', 12), ('gr', 14), ('sg', 6, 0), ('S', 6, 1), ('qr', 13), ('gr', 15), ('sg', 6, 1), ('S', 3, 0), ('qr', 14), ('sg', 0, 0), ('S', 3, 1), ('qr', 15), ('gfb',), ('sg', 0, 1), ('sg', 1, 0), ('sg', 1, 1), ('sg', 2, 0), ('sg', 2, 1), ('sg', 3, 0), ('sg', 3, 1), ('ln', 0), ('ln', 1), ('gd', 0, 0), ('gd', 0, 1), ('ln', 2), ('gn', 0), ('ln', 3), ('gd', 1, 0), ('gd', 1, 1), ('ln', 4), ('qf', 0), ('gd', 2, 0), ('F', 0, 0), ('gn', 1), ('gd', 2, 1), ('F', 0, 1), ('ln', 5), ('C', 0, 0), ('G', 4, 0), ('G', 4, 1), ('C', 0, 1), ('ln', 6), ('T', 0, 0), ('T', 0, 1), ('qf', 1), ('gd', 3, 0), ('F', 1, 0), ('gn', 2), ('gd', 3, 1), ('S', 8, 0), ('F', 1, 1), ('C', 1, 0), ('S', 8, 1), ('C', 1, 1), ('sg', 8, 0), ('T', 1, 0), ('sg', 8, 1), ('T', 1, 1), ('qf', 2), ('gd', 4, 0), ('S', 9, 0), ('gn', 3), ('S', 9, 1), ('sg', 9, 0), ('gd', 4, 1), ('F', 2, 0), ('sg', 9, 1), ('S', 10, 0), ('C', 2, 0), ('F', 2, 1), ('sg', 10, 0), ('S', 10, 1), ('C', 2, 1), ('S', 11, 0), ('sg', 10, 1), ('qf', 3), ('G', 5, 0), ('sg', 11, 0), ('G', 5, 1), ('gn', 4), ('gd', 5, 0), ('S', 11, 1), ('gd', 5, 1), ('S', 12, 0), ('sg', 11, 1), ('F', 3, 0), ('sg', 12, 0), ('S', 12, 1), ('C', 3, 0), ('F', 3, 1), ('sg', 12, 1), ('S', 7, 0), ('C', 3, 1), ('S', 7, 1), ('sg', 7, 0), ('qf', 4), ('G', 6, 0), ('sg', 7, 1), ('G', 6, 1), ('gn', 5), ('gd', 6, 0), ('F', 4, 0), ('gd', 6, 1), ('F', 4, 1), ('C', 4, 0), ('G', 8, 0), ('C', 4, 1), ('G', 8, 1), ('T', 2, 0), ('ln', 7), ('qf', 5), ('T', 2, 1), ('gn', 6), ('T', 3, 0), ('T', 3, 1), ('ln', 8), ('gd', 7, 0), ('T', 4, 0), ('T', 4, 1), ('gd', 7, 1), ('S', 14, 0), ('ln', 9), ('S', 14, 1), ('F', 5, 0), ('ln', 10), ('F', 5, 1), ('C', 5, 0), ('C', 5, 1), ('T', 5, 0), ('ln', 11), ('qf', 6), ('T', 5, 1), ('gd', 8, 0), ('gn', 7), ('F', 6, 0), ('gd', 8, 1), ('ln', 12), ('F', 6, 1), ('C', 6, 0), ('G', 9, 0), ('C', 6, 1), ('G', 9, 1), ('T', 6, 0), ('qf', 7), ('T', 6, 1), ('gd', 9, 0), ('F', 7, 0), ('gn', 8), ('gd', 9, 1), ('sg', 14, 0), ('F', 7, 1), ('C', 7, 0), ('sg', 14, 1), ('G', 10, 0), ('S', 15, 0), ('C', 7, 1), ('S', 15, 1), ('sg', 15, 0), ('G', 10, 1), ('qf', 8), ('sg', 15, 1), ('T', 7, 0), ('gd', 10, 0), ('gn', 9), ('T', 7, 1), ('gd', 10, 1), ('S', 13, 0), ('rt', 0, 0), ('S', 13, 1), ('sg', 13, 0), ('F', 8, 0), ('rt', 0, 1), ('sg', 13, 1), ('F', 8, 1), ('C', 8, 0), ('G', 11, 0), ('C', 8, 1), ('G', 11, 1), ('T', 8, 0), ('qf', 9), ('gd', 11, 0), ('T', 8, 1), ('gn', 10), ('F', 9, 0), ('ln', 13), ('gd', 11, 1), ('F', 9, 1), ('C', 9, 0), ('ln', 14), ('G', 12, 0), ('C', 9, 1), ('G', 12, 1), ('T', 9, 0), ('qf', 10), ('ln', 15), ('gd', 12, 0), ('T', 9, 1), ('gn', 11), ('F', 10, 0), ('gd', 12, 1), ('rb', 0, 0), ('F', 10, 1), ('C', 10, 0), ('G', 14, 0), ('C', 10, 1), ('G', 14, 1), ('T', 10, 0), ('qf', 11), ('T', 10, 1), ('gd', 13, 0), ('gn', 12), ('F', 11, 0), ('gd', 13, 1), ('F', 11, 1), ('C', 11, 0), ('B', 0, 0), ('C', 11, 1), ('T', 11, 0), ('ro', 0, 0), ('T', 11, 1), ('qf', 12), ('rb', 0, 1), ('B', 0, 1), ('gd', 14, 0), ('gn', 13), ('F', 12, 0), ('ro', 0, 1), ('gd', 14, 1), ('F', 12, 1), ('C', 12, 0), ('G', 15, 0), ('C', 12, 1), ('G', 15, 1), ('T', 12, 0), ('qf', 13), ('T', 12, 1), ('gd', 15, 0), ('gn', 14), ('F', 13, 0), ('gd', 15, 1), ('F', 13, 1), ('C', 13, 0), ('C', 13, 1), ('T', 13, 0), ('T', 13, 1), ('qf', 14), ('gn', 15), ('F', 14, 0), ('F', 14, 1), ('C', 14, 0), ('C', 14, 1), ('T', 14, 0), ('qf', 15), ('T', 14, 1), ('F', 15, 0), ('F', 15, 1), ('C', 15, 0), ('C', 15, 1), ('T', 15, 0), ('rt', 1, 0), ('T', 15, 1), ('rt', 1, 1), ('rb', 1, 0), ('B', 1, 0), ('ro', 1, 0), ('rb', 1, 1), ('B', 1, 1), ('qo', 0), ('ro', 1, 1), ('qo', 1)]
HELD = {0: "filt", 1: "acc", 2: "grd"}
VECTOR_GAIN = (0, 15)

FLOPS = 2 * 2048 * 512 * 1024 + 2 * 2048 * 1024 * 1024


def tile_schnetfilterinteraction_x2_kernel(
    tc, x, dist, mu, gr, w1_words, w1_scales, gf, w2_words, w2_scales, out_0, out_1, out_2
):
    nc = tc.nc
    with ExitStack() as ctx:
        keep = ctx.enter_context(tc.tile_pool(name="keep", bufs=1))
        work = ctx.enter_context(tc.tile_pool(name="work", bufs=3))
        psum = ctx.enter_context(tc.psum_pool(name="psum", bufs=2))
        ctx.enter_context(tc.manual_schedule(engines={ENG.Activation, ENG.DVE, ENG.Pool, ENG.SP, ENG.PE}))

        ident_bf = keep.tile([P, P], BF16)
        ident_f32 = keep.tile([P, P], F32)
        make_identity(nc, ident_bf[:])
        make_identity(nc, ident_f32[:])

        s1_raw = keep.tile([P, 1024], U8, align_bytes=64)
        s2 = keep.tile([P, 2, 1024], U8, align_bytes=64)
        d_feat = keep.tile([P, TILES * 8 + 120], BF16)
        mu_feat = keep.tile([P, 4, P], BF16)
        d_slots = d_feat[:, 0 : TILES * 8].rearrange("p (k f) -> p k f", f=8)
        nc.vector.memset(s1_raw[:].bitcast(I32), 0)
        nc.vector.memset(d_feat[:].bitcast(I32), 0)
        nc.vector.memset(mu_feat[:].rearrange("p t n -> p (t n)").bitcast(I32), 0)
        nc.vector.memset(s2[:].rearrange("p g n -> p (g n)").bitcast(I32), 0)
        nc.vector.memset(d_slots[:, :, 3:5], 1.0)
        nc.vector.memset(mu_feat[:, :, 1:3], 1.0)

        d_sb = keep.tile([P, TILES], BF16)
        mu_sb = keep.tile([P, 4], BF16)
        gr_sb = keep.tile([P, 4], BF16)
        gf_sb = keep.tile([P, 2, 4], BF16)
        w1_raw = keep.tile([P, 2048], U8, align_bytes=64)
        w2 = keep.tile([P, 2, 2048], U8, align_bytes=64)
        x_sb = keep.tile([P, ATOMS, 1024], BF16)
        nc.sync.dma_start(out=d_sb[:], in_=dist.rearrange("b i j -> (b i j)").rearrange("(p k) -> p k", k=TILES))
        nc.sync.dma_start(out=mu_sb[:], in_=mu.rearrange("(p t) -> p t", t=4))
        nc.sync.dma_start(out=gr_sb[:], in_=gr.rearrange("(p t) -> p t", t=4))
        for q in range(4):
            nc.sync.dma_start(
                out=s1_raw[32 * q : 32 * q + 4, :].bitcast(I32), in_=w1_scales[0, 4 * q : 4 * q + 4, :].bitcast(I32)
            )
        nc.sync.dma_start(out=w1_raw[:].bitcast(I32), in_=w1_words[0].bitcast(I32))
        nc.sync.dma_start(out=gf_sb[:], in_=gf.rearrange("(g p t) -> p g t", g=2, t=4))
        for q in range(4):
            nc.sync.dma_start(
                out=s2[32 * q : 32 * q + 4, :, :].bitcast(I32),
                in_=w2_scales[:, 4 * q : 4 * q + 4, :].rearrange("g r n -> r g n").bitcast(I32),
            )
        nc.sync.dma_start(out=w2[:].bitcast(I32), in_=w2_words.rearrange("g p n -> p g n").bitcast(I32))
        x_rows = x.rearrange("b j c -> b (j c)")
        x_flat = x_sb[:].rearrange("p j c -> p (j c)")
        for r in range(4):
            nc.sync.dma_start(out=x_flat[r:P:4, :], in_=x_rows)

        turns_int = keep.tile([P, TILES], I32)
        turns = keep.tile([P, TILES], F32)
        sine = keep.tile([P, TILES], F32)
        nc.vector.tensor_scalar(
            out=turns_int[:], in0=d_sb[:], scalar1=0.5 / CUTOFF, scalar2=None, op0=ALU.mult
        )
        d_sq = keep.tile([P, TILES], F32)
        mu_sq = keep.tile([P, 4], F32)
        nc.vector.tensor_tensor(out=d_sq[:], in0=d_sb[:], in1=d_sb[:], op=ALU.mult)
        nc.vector.scalar_tensor_tensor(
            out=turns[:], in0=d_sb[:], scalar=0.5 / CUTOFF, in1=turns_int[:], op0=ALU.mult, op1=ALU.subtract
        )
        nc.scalar.activation(out=sine[:], in_=turns[:], func=ACT.Sin, scale=math.pi)

        nc.vector.tensor_tensor(out=mu_sq[:], in0=mu_sb[:], in1=mu_sb[:], op=ALU.mult)
        nc.vector.tensor_copy(out=d_slots[:, :, 1], in_=d_sq[:])
        nc.vector.tensor_copy(out=mu_feat[:, :, 3], in_=mu_sq[:])
        nc.vector.tensor_copy(out=d_slots[:, :, 0], in_=d_sb[:])
        nc.vector.tensor_scalar(out=mu_feat[:, :, 0], in0=mu_sb[:], scalar1=-2.0, scalar2=None, op0=ALU.mult)
        nc.vector.tensor_tensor(out=mu_feat[:, :, 4], in0=mu_sq[:], in1=mu_feat[:, :, 3], op=ALU.subtract)
        nc.vector.tensor_tensor(out=d_slots[:, :, 2], in0=d_sq[:], in1=d_slots[:, :, 1], op=ALU.subtract)

        mu_rows = keep.tile([P, 4, P], BF16)
        d_rows = keep.tile([P, TILES, P], BF16)
        turned = psum.tile([P, 4, P], BF16, tag="grd", name="turned_mu")
        for t in range(4):
            nc.tensor.transpose(turned[:, t, :], mu_feat[:, t, :], ident_bf[:])
        nc.vector.tensor_copy(out=mu_rows[:], in_=turned[:])
        r_codes = keep.tile([P, TILES, P], U32, align_bytes=64)
        r_scales = keep.tile([P, TILES, P], U8, align_bytes=64)
        fc = keep.tile([P, TILES], F32)
        sine_sq = keep.tile([P, TILES], F32)
        neg_gf = keep.tile([P, 2, P, 4], BF16)
        plane_bf = keep.tile([P, 2, 2 * P, 4], BF16, align_bytes=64)
        codes = keep.tile([P, 2, 2 * P], U32, align_bytes=64)
        scales = keep.tile([P, 2, 2 * P], U8, align_bytes=64)
        out_rows = out_0.rearrange("b i c -> (b i) c").rearrange("(q h) c -> q h c", h=2)
        tl = {}

        def neg_h(k, g, tag):
            bank = psum.tile([P, 4, P], F32, tag=tag, name="neg_h")
            for t in range(4):
                nc.tensor.matmul_mx(
                    out=bank[:, t, :],
                    lhsT=w1[:, g, t, :].bitcast(FP4X4),
                    lhsT_scale=s1[:, g, t, :],
                    rhs=r_codes[:, k, :].bitcast(FP8X4),
                    rhs_scale=r_scales[:, k, :],
                    start=True,
                    stop=True,
                )
            tl["h", k, g] = bank[:].rearrange("p t n -> p n t")

        def emit(step, k=0, g=0):
            if step == "q":
                sq = psum.tile([P, 4, P], F32, tag="sig", name="sq")
                for t in range(4):
                    nc.tensor.matmul(sq[:, t, :], lhsT=mu_rows[:, t, :], rhs=d_rows[:, k, :], start=True, stop=True)
                tl["sq", k] = sq
            elif step == "E":
                rbf = work.tile([P, P, 4], F32, tag="rbf", bufs=TILES)
                nc.scalar.activation(
                    out=rbf[:], in_=tl["sq", k][:].rearrange("p t n -> p n t"), func=ACT.Exp, scale=-GAMMA
                )
                tl["rbf", k] = rbf
            elif step == "gr":
                r_bf = work.tile([P, 4 * P], BF16, tag="r_bf", align_bytes=64)
                nc.vector.tensor_tensor(
                    out=r_bf[:].rearrange("p (n t) -> p n t", t=4),
                    in0=tl["rbf", k][:],
                    in1=neg_gr[:].unsqueeze(1).to_broadcast([P, P, 4]),
                    op=ALU.mult,
                )
                tl["r_bf", k] = r_bf
                if k == TILES - 1:
                    nc.vector.tensor_tensor(out=sine_sq[:], in0=sine[:], in1=sine[:], op=ALU.mult)
            elif step == "qr":
                nc.vector.quantize_mx(
                    out=r_codes[:, k, :].bitcast(FP8X4), scales=r_scales[:, k, :], in_=tl["r_bf", k][:]
                )
            elif step == "gfb":
                inv_root = 1.0 / math.sqrt(ATOMS)
                nc.vector.tensor_scalar(
                    out=fc[:], in0=sine_sq[:], scalar1=-inv_root, scalar2=inv_root, op0=ALU.mult, op1=ALU.add
                )
                for u in range(2):
                    nc.vector.tensor_scalar(
                        out=neg_gf[:, u],
                        in0=gf_sb[:, u, :].unsqueeze(1).to_broadcast([P, P, 4]),
                        scalar1=-1.0,
                        scalar2=None,
                        op0=ALU.mult,
                    )
            elif step == "S":
                neg_h(k, g, HELD.get(k, "sig"))
            elif step == "G":
                neg_h(k, g, "grd")
            elif step == "sg":
                if g == 0:
                    tl["logs", k] = work.tile([P, 2, P, 4], F32, tag="logs", name="logs", bufs=TILES)
                nc.scalar.activation(out=tl["logs", k][:, g], in_=tl["h", k, g], func=ACT.Sigmoid)
            elif step == "ln":
                flat = tl["logs", k][:].rearrange("p g n t -> p (g n t)")
                nc.scalar.activation(out=flat, in_=flat, func=ACT.Ln, scale=2.0, bias=LN_FLOOR)
            elif step == "gd":
                if g == 0:
                    tl["m", k] = work.tile([P, 2, P, 4], F32, tag="neg_ssp", name="neg_ssp")
                nc.vector.scalar_tensor_tensor(
                    out=tl["m", k][:, g],
                    in0=tl["h", k, g],
                    scalar=LN2,
                    in1=tl["logs", k][:, g],
                    op0=ALU.add,
                    op1=ALU.min,
                )
            elif step == "gn":
                f_bf = work.tile([P, 1024], BF16, tag="f_bf", bufs=1, align_bytes=64)
                engine = nc.vector if k in VECTOR_GAIN else nc.gpsimd
                engine.tensor_tensor(
                    out=f_bf[:],
                    in0=tl["m", k][:].rearrange("p g n t -> p (g n t)"),
                    in1=neg_gf[:].rearrange("p g n t -> p (g n t)"),
                    op=ALU.mult,
                )
                tl["f_bf", k] = f_bf
            elif step == "qf":
                f_codes = work.tile([P, 2, P], U32, tag="f_codes", align_bytes=64)
                f_scales = work.tile([P, 2, P], U8, tag="f_scales", align_bytes=64)
                nc.vector.quantize_mx(
                    out=f_codes[:].rearrange("p g n -> p (g n)").bitcast(FP8X4),
                    scales=f_scales[:].rearrange("p g n -> p (g n)"),
                    in_=tl["f_bf", k][:],
                )
                tl["fq", k] = (f_codes, f_scales)
            elif step == "F":
                filt = psum.tile([P, 512], F32, tag="filt")
                f_codes, f_scales = tl["fq", k]
                for u in range(2):
                    nc.tensor.matmul_mx(
                        out=filt[:],
                        lhsT=f_codes[:, u, :].bitcast(FP8X4),
                        lhsT_scale=f_scales[:, u, :],
                        rhs=w2[:, u, 1024 * g : 1024 * (g + 1)].bitcast(FP4X4),
                        rhs_scale=s2[:, u, 512 * g : 512 * (g + 1)],
                        start=(u == 0),
                        stop=(u == 1),
                    )
                tl["filt", k, g] = filt
            elif step == "C":
                msg = work.tile([P, 4, P], F32, tag="msg", bufs=6)
                nc.vector.scalar_tensor_tensor(
                    out=msg[:],
                    in0=tl["filt", k, g][:].rearrange("q (p t) -> q t p", t=4),
                    scalar=fc[:, k : k + 1],
                    in1=x_sb[:, k % ATOMS, 512 * g : 512 * (g + 1)].rearrange("q (p t) -> q t p", t=4),
                    op0=ALU.mult,
                    op1=ALU.mult,
                )
                tl["msg", k, g] = msg
            elif step == "T":
                h, j = divmod(k, ATOMS)
                if j == 0:
                    tl["acc", h, g] = psum.tile([P, 4, P], F32, tag="acc", name="acc")
                for t in range(4):
                    nc.tensor.matmul(
                        tl["acc", h, g][:, t, :],
                        lhsT=tl["msg", k, g][:, t, :],
                        rhs=ident_f32[:],
                        is_transpose=True,
                        start=(j == 0 and t == 0),
                        stop=(j == ATOMS - 1 and t == 3),
                    )
            elif step == "rt":
                tl["sums", k, g] = keep.tile([P, 4, P], F32, name="sums_%d_%d" % (k, g))
                move = nc.scalar.copy if k == 1 else nc.vector.tensor_copy
                move(out=tl["sums", k, g][:], in_=tl["acc", k, g][:])
            elif step == "rb":
                move = nc.scalar.copy if k == 0 else nc.vector.tensor_copy
                move(
                    out=plane_bf[:, g].rearrange("p (q h) t -> p q h t", h=2)[:, :, k, :],
                    in_=tl["sums", k, g][:].rearrange("p t q -> p q t"),
                )
            elif step == "B":
                back = psum.tile([P, 4, P], F32, tag="sig")
                for t in range(4):
                    nc.tensor.transpose(back[:, t, :], tl["sums", k, g][:, t, :], ident_f32[:])
                tl["back", k, g] = back
            elif step == "ro":
                rows = work.tile([P, P, 4], F32, tag="rows", bufs=4)
                nc.scalar.copy(out=rows[:], in_=tl["back", k, g][:].rearrange("q t p -> q p t"))
                nc.sync.dma_start(
                    out=out_rows[:, k, 512 * g : 512 * (g + 1)], in_=rows[:].rearrange("q p t -> q (p t)")
                )
            elif step == "qo":
                nc.vector.quantize_mx(
                    out=codes[:, k, :].bitcast(FP8X4),
                    scales=scales[:, k, :],
                    in_=plane_bf[:, k].rearrange("p m t -> p (m t)"),
                )
                nc.sync.dma_start(
                    out=out_1[k].rearrange("p m t -> p (m t)").bitcast(I32), in_=codes[:, k, :].bitcast(I32)
                )

        for c, tag in enumerate(("filt", "filt", "acc", "acc")):
            turned = psum.tile([P, 4, P], BF16, tag=tag, name="turned_d")
            for u in range(4):
                k = 4 * c + u
                nc.tensor.transpose(turned[:, u, :], d_feat[:, 8 * k : 8 * k + P], ident_bf[:])
            nc.vector.tensor_copy(out=d_rows[:, 4 * c : 4 * c + 4, :], in_=turned[:])
            if c == 0:
                emit("q", 0)
                emit("q", 1)

        neg_gr = keep.tile([P, 4], F32)
        nc.vector.tensor_scalar(out=neg_gr[:], in0=gr_sb[:], scalar1=-1.0, scalar2=None, op0=ALU.mult)

        w1 = keep.tile([P, 2, 4, 256], U8, align_bytes=64)
        s1 = keep.tile([P, 2, 4, P], U8, align_bytes=64)
        for g in range(2):
            nc.vector.tensor_copy(
                out=w1[:, g].rearrange("p t (m e) -> p t m e", e=2),
                in_=w1_raw[:, 1024 * g : 1024 * (g + 1)].rearrange("p (m t e) -> p t m e", t=4, e=2),
            )
        nc.vector.tensor_copy(out=s1[:], in_=s1_raw[:].rearrange("p (g m t) -> p g t m", g=2, t=4))


        for item in ORDER[2:]:
            emit(*item)
        for q in range(4):
            nc.sync.dma_start(
                out=out_2[:, 4 * q : 4 * q + 4, :].rearrange("g r m -> r g m").bitcast(I32),
                in_=scales[32 * q : 32 * q + 4, :, :].bitcast(I32),
            )
